import numpy as np, ml_dtypes
CORES = [16,17,18,19,32,33,34,35]
N = 8
BF = ml_dtypes.bfloat16
def gentries(a):
    return np.ascontiguousarray(a.reshape(8, 16, -1).transpose(0, 2, 1)).reshape(8, -1)
def gtable(e):
    e = np.asarray(e); return np.ascontiguousarray(e.reshape(8, -1, 16).transpose(0, 2, 1)).reshape(128, -1).astype(np.int32)
V, B, CAP, D, VOTE, RO, ST = 1024, 128, 32, 4, 10, 3, 1024
def ranks():
    return np.arange(N).reshape(N, 1, 1, 1)
def heights(rng):
    b = rng.integers(0, 256, (N, 8, 1, V)); b[..., :B] += rng.choice(np.array([-30, 0, 40, 90]), (N, 8, 1, 1))
    return np.clip(b + rng.integers(-60, 61, (N, 8, 16, V)), 0, 255)
def weights(rng):
    return np.clip(rng.integers(0, 256, (N, 8, 1, D, V)) + rng.integers(-60, 61, (N, 8, 16, D, V)), 0, 255)
def names(rng):
    s = (N, 8, D, V); r = ranks()
    own = np.where(rng.random(s) < 0.5, (np.arange(V) + rng.integers(-24, 25, s)) % V, rng.integers(0, V, s))
    return np.where(rng.random(s) < 0.7, ST * r + own, ST * ((r + rng.integers(1, N, s)) % N) + rng.integers(0, B, s))
def pack(h, w, n):
    return {"h0": h.reshape(N, 128, V).astype(np.float32).astype(BF), "w0": w.reshape(N, 128, D * V).astype(np.float32).astype(BF), "nb": np.stack([gtable(a.reshape(8, -1)) for a in n])}
def setup_inputs(rng):
    h = heights(rng); w = weights(rng); n = names(rng)
    return pack(h, w, n)
def elsewhere(p):
    return np.concatenate([ST * q + np.arange(B) for q in range(N) if q != p])
def setup_inputs_room(rng):
    w = weights(rng); n = names(rng); h = np.zeros((N, 8, 16, V), np.int64); tops = np.zeros((N, 8, V), bool)
    for q in range(N):
        for g in range(8):
            k = int(rng.choice(np.array([0, 1, CAP - 1, CAP, CAP + 1, B])))
            if q < 2: k = (CAP, CAP + 1, B, CAP - 1, 1, 0, CAP, CAP + 1)[(g + 3 * q) % 8]
            top = np.zeros(V, bool); top[rng.permutation(B)[:k]] = True; top[B + rng.permutation(V - B)[:(V - B) // 4]] = True
            inner = B + np.flatnonzero(top[B:]); low = B + np.flatnonzero(~top[B:]); tops[q, g] = top
            h[q, g] = np.where(top, rng.integers(160, 256, (16, V)), rng.integers(0, 120, (16, V)))
            n[q, g] = np.where(top, ST * q + rng.choice(low, (D, V)), n[q, g])
            n[q, g, D - 1] = np.where(top, n[q, g, D - 1], ST * q + rng.choice(inner, V))
    a, b = [int(x) for x in 2 + rng.permutation(N - 2)[:2]]
    dead = np.concatenate([ST * q + np.flatnonzero(tops[q, 0, :B])[:CAP] for q in range(N) if q != a])
    h[a, 0] = rng.integers(0, 120, (16, V)); w[a, 0, :, 0] = rng.integers(200, 256, (16, V))
    n[a, 0, 0] = rng.choice(dead, V)
    n[a, 0, 1:] = rng.permutation(np.resize(elsewhere(a), (D - 1) * V)).reshape(D - 1, V)
    h[b, 1] = np.where(rng.random(V) < 0.5, rng.integers(245, 256, (16, V)), rng.integers(0, 120, (16, V)))
    n[b, 1] = rng.permutation(np.resize(elsewhere(b), D * V)).reshape(D, V)
    low = rng.permutation(B)[CAP:]; top = np.ones(V, bool); top[low] = False
    h[a, 2] = np.where(top, rng.integers(160, 256, (16, V)), rng.integers(0, 120, (16, V)))
    t = ST * a + rng.choice(low, (D, V)); t[:, low] = ST * a + rng.integers(B, V, (D, low.size)); t[0, low] = ST * a + V - 1 - rng.permutation(low.size)
    n[a, 2] = t
    return pack(h, w, n)
def setup_inputs_ties(rng):
    n = names(rng); me = ST * ranks() + np.arange(V)
    c = rng.choice(np.array([0, 0, 0, 0, 0, 0, 0, VOTE - 1, VOTE, VOTE, 16]), (N, 8, 1, V))
    h = rng.integers(20, 200, (1, 8, 1, 1)) + (np.argsort(rng.random((N, 8, 16, V)), axis=2) < c)
    w = rng.choice(np.array([0, 60, 120, 180]), (N, 8, 1, D, V)) + 3 * ((np.arange(16).reshape(16, 1, 1) + rng.integers(0, 16, (N, 8, 1, D, V))) % 16)
    n[:, :, 1] = np.where(rng.random((N, 8, V)) < 0.3, n[:, :, 0], n[:, :, 1])
    n[:, :, D - 1] = np.where(rng.random((N, 8, V)) < 0.2, n[:, :, 0], n[:, :, D - 1])
    n = np.where(rng.random(n.shape) < 0.1, me, n)
    return pack(h, w, n)
def late(rng, h, n, g):
    s = (D, V)
    for q in range(N):
        o = B + rng.permutation(V - B); y, z = int(o[0]), int(o[1]); low = np.concatenate([np.arange(B), o[2:]])
        h[q, g] = rng.integers(0, 120, (16, V)); h[q, g, :, z] = rng.integers(150, 190, 16); h[q, g, :, y] = rng.integers(200, 256, 16)
        t = np.where(rng.random(s) < 0.7, ST * q + rng.choice(low, s), ST * ((q + rng.integers(1, N, s)) % N) + rng.integers(0, B, s))
        l = rng.integers(0, D, V); t[l, np.arange(V)] = ST * q + z; t[l[z], z] = ST * q + y
        n[q, g] = t
def setup_inputs_alike(rng):
    h = heights(rng) // 2; w = weights(rng); n = names(rng); r = ranks(); s = (N, 4, D, V); hub = np.array([0, B - 1, V - 1])
    mine = ST * r + rng.choice(hub, s); far = ST * ((r + rng.integers(1, N, s)) % N) + rng.choice(hub[:2], s)
    n[:, 1::2] = np.where(rng.random(s) < 0.5, mine, far)
    n[:, ::4] = np.array(n[:, ::4, :1])
    h[..., hub] = rng.integers(200, 256, (N, 8, 16, 3)); n[..., hub] = ST * r + rng.integers(B, V - 1, (N, 8, D, 3))
    late(rng, h, n, int(rng.choice(np.array([2, 6]))))
    return pack(h, w, n)
def setup_inputs_bare(rng):
    h = heights(rng); w = weights(rng); n = names(rng); r = ranks(); me = ST * r + np.arange(V); nx = ST * r + (np.arange(V) + 1) % V
    n = np.where(rng.random(n.shape) < 0.4, me, n); g = rng.permutation(8); q = rng.permutation(N)
    h[:, g[0]] = 77; n[:, g[0]] = np.where(n[:, g[0]] == me[:, 0], nx[:, 0], n[:, g[0]])
    n[q[0], g[1]] = me[q[0], 0]
    w[:, g[2]] = 0
    return pack(h, w, n)
def setup_inputs_spread(rng):
    h = (np.exp2(8 * rng.random((N, 8, 1, V))) * rng.random((N, 8, 16, V))).astype(np.int64)
    w = np.minimum((2 * np.exp2(8 * rng.random((N, 8, 1, D, V))) * rng.random((N, 8, 16, D, V))).astype(np.int64), 255)
    s = (N, 8, D, V); r = ranks(); u = rng.random(s) ** 3
    n = np.where(rng.random(s) < 0.6, ST * r + (V * u).astype(np.int64), ST * ((r + rng.integers(1, N, s)) % N) + (B * u).astype(np.int64))
    return pack(h, w, n)
def check_inputs(d):
    bad = []
    for k in ("h0", "w0"):
        a = np.asarray(d[k]).astype(np.float64)
        if not np.all((a >= 0) & (a <= 255) & (a == np.floor(a))): bad.append("whole numbers from 0 to 255 in " + k)
    e = np.stack([gentries(a) for a in d["nb"]]).astype(np.int64); q = e // ST; v = e - ST * q
    if not np.all((q >= 0) & (q < N) & (v < np.where(q == np.arange(N).reshape(N, 1, 1), V, B))): bad.append("names in nb")
    return bad
def reference(h0, w0, nb):
    h = h0.astype(np.float32).astype(np.int32).reshape(N, 8, 16, V); w = w0.astype(np.float32).astype(np.int32).reshape(N, 8, 16, D, V)
    m = np.stack([gentries(a) for a in nb]).astype(np.int64).reshape(N, 8, D, V); m = (m // ST) * V + m % ST
    live = np.ones((N, 8, V), bool); rising = (2 * D - 1 - np.arange(2 * D)).reshape(2 * D, 1)
    for rnd in range(RO):
        hg = h.transpose(1, 2, 0, 3).reshape(8, 16, N * V); wg = w.transpose(1, 2, 3, 0, 4).reshape(8, 16, D, N * V); mg = m.transpose(1, 2, 0, 3).reshape(8, D, N * V)
        die = []
        for r in range(N):
            a = np.take_along_axis(hg, m[r].reshape(8, 1, D * V), 2).reshape(8, 16, D, V)
            votes = np.add.reduce((h[r][:, :, None, :] > a).astype(np.int32), axis=1)
            die.append(np.all((votes >= VOTE) | (m[r] == r * V + np.arange(V)), axis=1))
        die = np.stack(die) & live
        e = die[:, :, :B].astype(np.int64); before = np.add.accumulate(e, axis=2) - e
        die[:, :, :B] = (e == 1) & (before < CAP)
        live = live & ~die; dg = die.transpose(1, 0, 2).reshape(8, N * V)
        hn, wn, mn = [], [], []
        for r in range(N):
            me = r * V + np.arange(V)
            gone = np.take_along_axis(dg, m[r].reshape(8, D * V), 1).reshape(8, D, V)
            hit = live[r] & np.any(gone, axis=1)
            s = np.argmax(gone, axis=1)[:, None, :]; d = np.take_along_axis(m[r], s, 1)
            ws = np.take_along_axis(w[r], s[:, None], 2)
            wd = np.take_along_axis(wg, d[:, None], 3); hd = np.take_along_axis(hg, d, 2)[:, :, None, :]
            cw = np.concatenate([w[r], np.clip(ws + wd - hd, 0, 255)], axis=2)
            cm = np.concatenate([m[r], np.take_along_axis(mg, d, 2)], axis=1)
            q = cm // V; v = cm - q * V
            out = (cm == me) | np.take_along_axis(dg, cm.reshape(8, -1), 1).reshape(cm.shape) | ((q != r) & (v >= B))
            key = np.where(out, -1, 2 * D * np.add.reduce(cw, axis=1) + rising)
            twin = np.any((cm[:, :, None] == cm[:, None]) & (key[:, :, None] > key[:, None]), axis=1)
            key = np.where(twin, -1, key)
            o = np.argsort(-key, axis=1, kind="stable")[:, :D]; full = np.take_along_axis(key, o, 1) >= 0
            nm = np.where(full, np.take_along_axis(cm, o, 1), me); nw = np.where(full[:, None], np.take_along_axis(cw, o[:, None], 2), 0)
            mn.append(np.where(hit[:, None], nm, m[r])); wn.append(np.where(hit[:, None, None], nw, w[r]))
            hn.append(np.where(hit[:, None], (h[r] + np.maximum(h[r], ws[:, :, 0])) >> 1, h[r]))
        h, w, m = np.stack(hn), np.stack(wn), np.stack(mn)
    m = (m // V) * ST + m % V
    return {"yh": h.reshape(N, 128, V).astype(np.float32).astype(BF), "yw": w.reshape(N, 128, D * V).astype(np.float32).astype(BF), "yn": np.stack([gtable(a.reshape(8, -1)) for a in m]).astype(np.float32)}

@@ -1,0 +1,716 @@
+from concourse.bass import DstId, RemoteDMATransfer
+from concourse.mybir import AluOpType, ActivationFunctionType
+
+A = AluOpType
+F = ActivationFunctionType
+RO = 3
+BIG = float(2 ** 25)
+RK = float(2 ** 19)
+MODE = "bbbb"
+ASR = ("vvss", "vvvv", "vvvv")
+GS = ("vvvv", "vvss", "vvss")
+TB = "vs"
+SG = ((0, 1), (1, 3), (3, 7))
+BONUS = {"OP": 6000, "OG": 3000, "NAT": 2000}
+
+SCRATCH = {}
+
+
+def _sb(n, w, d):
+    SCRATCH[n] = ("sbuf", [128, w], d)
+
+
+def _su(n, u, d):
+    SCRATCH[n] = ("sbuf", [128, u, 64], d)
+
+
+for _i in range(8):
+    SCRATCH["pb%d" % _i] = ("psum", [128, 8, 64], "float32")
+for _i in range(RO):
+    _sb("H%d" % _i, 4096, "bfloat16")
+    _sb("TAB%d" % _i, 2048, "bfloat16")
+for _i in range(RO + 1):
+    _sb("HO%d" % _i, 1024, "bfloat16")
+for _n, _w in (("PL0", 12288), ("PL1", 12288), ("CMP", 4096), ("G", 4096), ("WD", 4096), ("NAT", 1024), ("IG", 1024), ("WS", 1024),
+               ("NE", 1024), ("Q", 1024), ("FB", 128), ("JUNK", 128), ("DN", 144), ("DT", 144), ("DS", 144), ("DA", 144), ("DR", 576),
+               ("WP", 2304), ("BL", 128), ("ID", 128), ("IN", 128), ("IH", 128), ("KP", 128), ("KN", 128), ("RP", 128), ("RN", 128),
+               ("I4", 128), ("IC", 128), ("D", 144), ("DH", 144), ("HP", 128), ("HM", 128), ("HN", 1792)):
+    _sb(_n, _w, "bfloat16")
+for _n, _w in (("J", 144), ("JG", 128), ("JR", 128), ("COL", 32), ("EQ", 16), ("WR", 16), ("C8", 4), ("WOULD", 128), ("CUM", 128),
+               ("PA", 128), ("DB", 128), ("ONE", 128), ("ACC", 8)):
+    _sb(_n, _w, "float32")
+_sb("KC", 8, "int32")
+_sb("NB", 256, "int32")
+_sb("YN", 256, "float32")
+for _n, _w in (("OA", 256), ("OG", 256), ("OP", 256), ("OW", 256), ("OS", 64), ("OD", 64), ("OI", 64), ("OC", 8)):
+    _sb(_n, _w, "uint16")
+for _n, _u in (("N8", 8), ("S16", 4), ("AI", 4), ("RI", 4), ("NM", 4), ("T4", 4), ("U4", 4), ("W4", 4), ("SI", 8), ("VI", 4), ("PRI", 4)):
+    _su(_n, _u, "int32")
+for _n, _u in (("KS", 8), ("Z", 8), ("SP", 4), ("X", 4), ("SM", 16), ("ME", 4), ("V4", 4), ("EMP", 4), ("FILL", 4),
+               ("AS", 16), ("L1", 8), ("L2", 4), ("NL", 1), ("PT", 4)):
+    _su(_n, _u, "float32")
+for _n, _u in (("P1", 8), ("P2", 8), ("FL", 8), ("F2", 8), ("V3", 4), ("SB", 4), ("CB", 8), ("CC", 8), ("KF", 8), ("O1", 28), ("O2", 28),
+               ("O3", 28), ("O4", 28)):
+    _su(_n, _u, "bfloat16")
+
+SEMAPHORES = ["qv", "qs", "qt", "qg"] + ["d%d" % _i for _i in range(24)]
+for _i in range(3 * RO):
+    SEMAPHORES += ["xa%d" % _i, "xb%d" % _i, "xl%d" % _i, "xf%d" % _i]
+
+
+def build(T, topo, core):
+    me = T.rank_of(core)
+    ops = []
+
+    def R(n, lo, hi, st=1):
+        return (T[n][:, lo:hi:st] if st > 1 else T[n][:, lo:hi], [(n, lo, hi, st, lo % st)], (hi - lo + st - 1) // st, n)
+
+    def U(n, a, b=None, st=1):
+        b = a + 1 if b is None else b
+        return (T[n][:, a:b:st, :] if st > 1 else T[n][:, a:b, :], [(n, 64 * a, 64 * b, st, a % st)], 64 * ((b - a + st - 1) // st), n)
+
+    def P(bank, a, b=None, st=1):
+        return U("pb%d" % bank, a, b, st)
+
+    def IND(win, off):
+        return (win[0].indirect(off[0]), win[1] + off[1], 16 * off[2], None)
+
+    def fp(*xs):
+        r = []
+        for x in xs:
+            if isinstance(x, tuple):
+                r += x[1]
+        return r
+
+    def val(x):
+        return x[0] if isinstance(x, tuple) else x
+
+    def span(o, a, k=None):
+        if a[3] is None:
+            return 60 + 1.55 * a[2]
+        if k is None:
+            k = 0.5 if SCRATCH[o[3]][2] == SCRATCH[a[3]][2] == "bfloat16" else 1.0
+        return 60 + 1.04 * max(64, k * a[2])
+
+    def add(q, fn, rd, wr, ns, kind="c", extra=None):
+        ops.append({"q": q, "fn": fn, "rd": rd, "wr": wr, "ns": ns, "kind": kind, "extra": extra})
+
+    def tt(o, a, b, op):
+        k = 1.0 if (str(a[3]).startswith("pb") or b[3].startswith("pb")) else 2.0
+        add("v", lambda e: e.tensor_tensor(o[0], a[0], b[0], op), fp(a, b), fp(o), span(o, a, k))
+
+    def ts(o, a, s1, op0, s2=None, op1=None):
+        if op1 is None:
+            add("v", lambda e: e.tensor_scalar(o[0], a[0], val(s1), None, op0), fp(a, s1), fp(o), span(o, a))
+        else:
+            add("v", lambda e: e.tensor_scalar(o[0], a[0], val(s1), val(s2), op0, op1), fp(a, s1, s2), fp(o), span(o, a))
+
+    def cp(o, a):
+        add("v", lambda e: e.tensor_copy(o[0], a[0]), fp(a), fp(o), span(o, a))
+
+    def ms(o, c):
+        add("v", lambda e: e.memset(o[0], c), [], fp(o), span(o, o))
+
+    def act(o, a, f=F.Identity, bias=0.0, scale=1.0, acc=None):
+        if acc is None:
+            add("s", lambda e: e.activation(o[0], a[0], f, bias=val(bias), scale=val(scale)), fp(a, bias, scale), fp(o), span(o, a, 1.0))
+        else:
+            add("s", lambda e: e.activation(o[0], a[0], f, bias=val(bias), scale=val(scale), accum_out=acc[0]),
+                fp(a, bias, scale), fp(o, acc), span(o, a, 1.0))
+
+    def mm(o, l, r, st=True, sp=True):
+        add("t", lambda e: e.matmul(o[0], l[0], r[0], st, sp), fp(l, r), fp(o), 0.55 * max(64, r[2]))
+
+    def iota(o, pat, base, cm, small=False):
+        if small:
+            add("g", lambda e: e.iota(o[0], pat, base, cm, allow_small_or_imprecise_dtypes=True), [], fp(o), 130 + 2.1 * o[2])
+        else:
+            add("g", lambda e: e.iota(o[0], pat, base, cm), [], fp(o), 130 + 2.1 * o[2])
+
+    nd = [0]
+
+    def dma(q, o, a, ns=2500):
+        s = "d%d" % nd[0]
+        nd[0] += 1
+        add(q, lambda e: e.dma_start(o[0], a[0]), fp(a), fp(o), ns, "d", s)
+
+    def X(ap):
+        return (ap, [])
+
+    mine = [q for q, c in enumerate(T.cores) if topo.chip(c) == topo.chip(core)]
+    other = [q for q, c in enumerate(T.cores) if topo.chip(c) != topo.chip(core)]
+    partner = other[mine.index(me)]
+    mates = [q for q in mine if q != me]
+    far = topo.mask(core, T.cores[partner])
+    near = topo.mask(core, T.cores[mates[0]])
+    rest = near & ~far
+
+    def cnt(m):
+        return bin(m).count("1")
+
+    def dst(q):
+        a = topo.addr(T.cores[q])
+        return DstId(rid=a[0], pnc=a[1])
+
+    nx = [0]
+
+    def send(buf, base, w, src=None):
+        i = nx[0]
+        nx[0] += 1
+        xa, xb, xl, xf = ("xa%d" % i, "xb%d" % i, "xl%d" % i, "xf%d" % i)
+
+        def slot(q):
+            return R(buf, base + w * q, base + w * (q + 1))
+        own = slot(me)
+        src = own if src is None else src
+        par = slot(partner)
+
+        def f1(e):
+            return e.remote_dma_fused([
+                RemoteDMATransfer(dst_ids=[dst(partner)], dma_engine_mask=far, remote_sem=T.sem[xa], srcs=[src[0]], dsts=[own[0]]),
+                RemoteDMATransfer(dst_ids=[dst(q) for q in mates], dma_engine_mask=rest, remote_sem=T.sem[xb], srcs=[src[0]],
+                                  dsts=[own[0] for q in mates])], local_sem=T.sem[xl])
+
+        def f2(e):
+            return e.remote_dma_fused([
+                RemoteDMATransfer(dst_ids=[dst(q) for q in mates], dma_engine_mask=near, remote_sem=T.sem[xb], srcs=[par[0]],
+                                  dsts=[par[0] for q in mates])], local_sem=T.sem[xf])
+        add("g", f1, fp(src), [], 3000, "r", (xl, cnt(far) + cnt(rest)))
+        add(None, None, [], fp(par), len(ops) - 1, "a", (xa, cnt(far)))
+        add("g", f2, fp(par), [], 3000, "r", (xf, cnt(near)))
+        add(None, None, [], fp(*[slot(q) for q in range(len(T.cores)) if q not in (me, partner)]), len(ops) - 1, "a",
+            (xb, len(mates) * (cnt(rest) + cnt(near))))
+
+    def sel(n, base, p):
+        return R(n, base + 15 - p, base + 143 - p)
+
+    def every16(src, lo, hi, p):
+        return (T[src][:, lo + p:hi:16], [(src, lo, hi, 1, 0)], (hi - lo) // 16, src)
+
+    def to_list(o, n, base, src, lo, hi):
+        for p in range(16):
+            mm(o, sel(n, base, p), every16(src, lo, hi, p), p == 0, p == 15)
+
+    def col(i):
+        return R("COL", i, i + 1)
+
+    def eye(n):
+        return R(n, 0, 128)
+
+    own0 = 1024 + 128 * me
+    dma("y", R("H0", own0, own0 + 128), X(T.h0[:, 0:128]))
+    dma("s", R("NB", 0, 256), X(T.nb[:]))
+    dma("y", R("H0", 0, 1024), X(T.h0[:]))
+    dma("y", R("HO0", 0, 1024), X(T.h0[:]))
+    iota(R("KC", 0, 1), [[0, 1]], 0, 1)
+    iota(R("J", 0, 144), [[1, 144]], 0, 0, True)
+    iota(U("VI", 0, 4), [[0, 4], [16, 64]], 0, 0)
+    at = len(ops)
+    iota(R("JG", 0, 128), [[16, 8], [0, 16]], 0, 0, True)
+    iota(R("JR", 0, 128), [[0, 8], [1, 16]], 0, 0, True)
+    iota(U("PRI", 0, 4), [[1, 4], [0, 64]], 0, 0)
+    early = ops[at:]
+    del ops[at:]
+    send("H0", 1024, 128)
+    ops[at + 2:at + 2] = early
+    ops[-1]["ns"] = len(ops) - 2
+    iota(U("CB", 0, 8), [[1, 8], [0, 64]], 1, 0, True)
+    iota(U("CC", 0, 4), [[2, 4], [0, 64]], -7, 0, True)
+    iota(U("CC", 4, 8), [[2, 4], [0, 64]], -1, 0, True)
+    ms(R("H0", 2048, 4096), -1.0)
+    ts(R("KC", 1, 2), R("KC", 0, 1), 15, A.bitwise_and)
+    cp(R("COL", 0, 2), R("KC", 0, 2))
+    tt(col(2), col(0), col(1), A.subtract)
+    ts(col(3), col(2), 15.0, A.add)
+    ts(col(4), col(1), 4.0, A.is_lt)
+    ts(R("EQ", 0, 16), R("J", 0, 16), col(1), A.is_equal)
+    ts(R("D", 0, 144), R("J", 0, 144), col(3), A.is_equal)
+    ts(col(7), col(4), 10.0, A.mult)
+    tt(col(5), col(7), R("EQ", 5, 6), A.add)
+    bias = []
+    for r in range(RO):
+        c = col(7)
+        for l in range(4):
+            if ASR[r][l] == "s":
+                ts(col(16 + r), R("EQ", l, l + 1), -8.0, A.mult, c, A.add)
+                c = col(16 + r)
+        bias.append(c)
+    act(R("DN", 0, 144), R("D", 0, 144), scale=-1.0)
+    ts(U("T4", 0, 4), R("NB", 0, 256), 3, A.arith_shift_right, 896, A.bitwise_and)
+    ts(U("U4", 0, 4), R("NB", 0, 256), 1023, A.bitwise_and)
+    ts(U("V4", 0, 4), U("VI", 0, 4), col(1), A.add)
+    ts(P(0, 0, 4), U("T4", 0, 4), 1024.0, A.add)
+    ts(U("W4", 0, 4), U("U4", 0, 4), 128.0, A.is_lt)
+    ts(P(1, 0, 4), U("V4", 0, 4), 128.0, A.is_lt, float(own0), A.mult)
+    tt(P(0, 4, 8), P(0, 0, 4), U("W4", 0, 4), A.mult)
+    tt(P(1, 4, 8), P(1, 0, 4), U("V4", 0, 4), A.add)
+    tt(U("N8", 0, 4), P(0, 4, 8), U("U4", 0, 4), A.add)
+    tt(U("T4", 0, 4), P(1, 4, 8), U("N8", 0, 4), A.is_equal)
+    ts(P(0, 0, 4), U("T4", 0, 4), 2048.0, A.mult)
+    tt(U("AI", 0, 4), P(0, 0, 4), U("N8", 0, 4), A.add)
+    cp(R("OA", 0, 256), U("AI", 0, 4))
+    act(U("ME", 0, 4), P(1, 4, 8))
+    act(U("EMP", 0, 4), P(1, 4, 8), bias=2048.0 + 2 ** 17 + 2 ** 16)
+    ts(R("PA", 0, 128), R("JR", 0, 128), 4.0, A.is_equal)
+    ts(col(6), R("EQ", 5, 6), -64.0, A.mult)
+    ts(col(8), col(4), 127.0, A.mult, col(6), A.add)
+    ts(R("PA", 0, 128), R("PA", 0, 128), col(8), A.mult, col(4), A.add)
+    ts(R("WOULD", 0, 128), R("JG", 0, 128), col(2), A.is_equal)
+    tt(R("BL", 0, 128), R("WOULD", 0, 128), R("PA", 0, 128), A.mult)
+    ts(eye("ID"), R("J", 0, 128), col(0), A.is_equal)
+    ms(R("ONE", 0, 128), 1.0)
+    ms(R("DB", 0, 128), 0.0)
+    ms(U("NL", 0), 0.0)
+    ts(col(9), col(1), -31.5, A.add)
+    ts(col(10), col(1), -15.5, A.add)
+    ts(col(11), R("EQ", 4, 5), 65536.0, A.mult)
+    ts(col(12), col(4), -2.0 * BIG, A.mult, col(11), A.add)
+    ts(R("WR", 8, 12), R("EQ", 8, 12), 16384.0, A.mult)
+    ts(R("C8", 0, 4), R("J", 0, 4), 2048.0, A.mult, 128.0, A.add)
+    tt(R("WR", 4, 8), R("EQ", 4, 8), R("EQ", 0, 4), A.add)
+    ts(U("PRI", 0, 4), U("PRI", 0, 4), float(4096 - 2 ** 22), A.mult, float(3 * 2 ** 22 + 4096 + 32 * 65536), A.add)
+    tt(R("WR", 0, 4), R("WR", 4, 8), R("WR", 8, 12), A.add)
+    ms(R("PL0", 0, 128), 0.0)
+    ms(R("PL1", 0, 128), 0.0)
+    ms(R("PL0", 3072, 4096), 0.0)
+    for p in range(16):
+        act(R("WP", 144 * p, 144 * p + 144), R("D", 0, 144), scale=R("EQ", p, p + 1))
+    act(R("DH", 0, 144), R("D", 0, 144), scale=-0.5)
+    act(R("DT", 0, 144), R("D", 0, 144), scale=col(12))
+    act(R("DA", 0, 144), R("D", 0, 144), scale=col(4))
+    act(R("DS", 0, 144), R("D", 0, 144), scale=4096.0)
+    for l in range(4):
+        act(R("DR", 144 * l, 144 * l + 144), R("D", 0, 144), scale=R("WR", l, l + 1))
+    for n, s in (("IN", -1.0), ("IH", 0.5), ("KP", BIG), ("KN", -BIG), ("HP", BIG / 2), ("HM", -BIG / 2), ("RP", RK), ("RN", -RK),
+                 ("I4", 4096.0), ("IC", RK + 4096.0)):
+        act(eye(n), eye("ID"), scale=s)
+    add("y", None, fp(R("H0", 1024, 2048)), [], 0, "w")
+    dma("y", R("PL0", 4096, 8192), X(T.w0[:]), 6000)
+    dma("y", R("H1", 2048, 4096), R("H0", 2048, 4096))
+    dma("y", R("H2", 2048, 4096), R("H0", 2048, 4096))
+    dma("y", R("PL1", 3072, 4096), R("PL0", 3072, 4096))
+    ID, IN, KP, KN = eye("ID"), eye("IN"), eye("KP"), eye("KN")
+    halves = ((128, 576), (576, 1024))
+    off = [0]
+    for d in range(1, 8):
+        off.append(off[-1] + 8 - d)
+
+    def pieces(a):
+        cp(U("P1", a, a + 4), U("N8", a, a + 4))
+        tt(U("P2", a, a + 4), U("N8", a, a + 4), U("P1", a, a + 4), A.subtract)
+
+    def sums(c, src, lo):
+        for p in range(16):
+            mm(P(3, c), sel("DS", 0, p), every16(src, lo, lo + 1024, p), p == 0, False)
+        mm(P(3, c), KP, U("P2", c), False, False)
+        mm(P(3, c), KP, U("P1", c), False, True)
+
+    for r in range(RO):
+        H, HX, HO, HN, TAB = "H%d" % r, "H%d" % (r + 1), "HO%d" % r, "HO%d" % (r + 1), "TAB%d" % r
+        PL, PX = "PL%d" % (r % 2), "PL%d" % ((r + 1) % 2)
+        HW = R(H, 0, 4096)
+        last = r == RO - 1
+        ASL = ASR[r]
+        for l in range(4):
+            tt(R("CMP", 1024 * l, 1024 * l + 128), IND(HW, R("OA", 64 * l, 64 * l + 8)), R(HO, 0, 128), A.is_lt)
+        for l in range(4):
+            mm(P(4, 0, 2), sel("DN", 0, l), R("CMP", 1024 * l, 1024 * l + 128), l == 0, l == 3)
+        act(R("FB", 0, 128), P(4, 0, 2), F.Relu, bias=col(5))
+        mm(P(4, 2, 4), R("BL", 0, 128), R("FB", 0, 128))
+        tt(R("WOULD", 0, 128), P(4, 2, 4), R("DB", 0, 128), A.is_le)
+        add("v", lambda e: e.tensor_tensor_scan(T.CUM[:, :], T.ONE[:, :], T.WOULD[:, :], -32.0, A.mult, A.add),
+            fp(R("ONE", 0, 128), R("WOULD", 0, 128)), fp(R("CUM", 0, 128)), 200)
+        tt(R(TAB, own0, own0 + 128), R("CUM", 0, 128), P(4, 2, 4), A.max)
+        send(TAB, 1024, 128)
+        cp(R("OG", 0, 256), U("N8", 0, 4))
+        pieces(0)
+        for h in range(2):
+            for p in range(8 * h, 8 * h + 8):
+                for f in range(8):
+                    mm(P(6 + h, p % 8), sel("WP", 144 * p, f), U("P%d" % (1 + f // 4), f % 4), f == 0, f == 7)
+            for p in range(8 * h, 8 * h + 8):
+                act(R("NAT", p, 1024, 16), P(6 + h, p % 8))
+        seq = [l for l in range(4) if ASL[l] == "v"]
+        seq = seq[:-1] + [l for l in range(4) if ASL[l] == "s"] + seq[-1:]
+        for h, (a, b) in enumerate(halves):
+            for n, l in enumerate(seq):
+                c, src = R("CMP", 1024 * l + a, 1024 * l + b), IND(HW, R("OA", 64 * l + a // 16, 64 * l + b // 16))
+                if ASL[l] == "v":
+                    tt(c, src, R(HO, a, b), A.is_lt)
+                else:
+                    hn = R("HN", 896 * (l % 2) + a - 128, 896 * (l % 2) + b - 128)
+                    act(hn, src)
+                    mm(P(2 + l % 2, 0, 7), ID, R(HO, a, b), True, False)
+                    mm(P(2 + l % 2, 0, 7), IN, hn, False, True)
+                    act(c, P(2 + l % 2, 0, 7), F.Sign, bias=-0.5)
+                mm(P(h, 0, 7), sel("DN" if ASL[l] == "v" else "DH", 0, l), c, n == 0, n == 3)
+        for h in range(2):
+            act(R("JUNK", 0, 128), R("CUM", 0, 128), F.Sign, bias=col(9 + h), scale=-1.0, acc=R("ACC", 4 * h, 4 * h + 1))
+        act(R(TAB, 0, 128), R(TAB, own0, own0 + 128))
+        for h in range(2):
+            ts(R("OC", h, 8, 2), R("C8", 0, 4), R("ACC", 4 * h, 4 * h + 1), A.add, 0.5, A.mult)
+        if not last:
+            ts(R("PA", 0, 128), R(TAB, own0, own0 + 128), -1.0, A.add, 1000.0, A.mult)
+            tt(R("DB", 0, 128), R("PA", 0, 128), R("DB", 0, 128), A.min)
+        for h, (a, b) in enumerate(halves):
+            if TB[h] == "v":
+                ts(R(TAB, a, b), P(h, 0, 7), bias[r], A.add, 0.0, A.max)
+            else:
+                act(R(TAB, a, b), P(h, 0, 7), F.Relu, bias=bias[r])
+        e3 = 1024 + 256 * me
+        act(R(PL, e3 + 128, e3 + 256), IND(R(PL, 4096, 8192), R("OC", 0, 8)))
+        to_list(P(4, 4), "DT", 0, TAB, 0, 1024)
+        tt(U("SP", 0, 4), U("N8", 0, 4), U("PRI", 0, 4), A.add)
+        ts(U("FL", 0, 4), U("AI", 0, 4), 2048.0, A.is_ge)
+        ts(U("SM", 15), P(4, 4), -BIG, A.is_gt, BIG, A.mult)
+        tt(U("NL", 0), U("NL", 0), U("SM", 15), A.max)
+        for l in range(4):
+            sums(l, PL, 4096 + 1024 * l)
+        act(U("Z", 0, 4), P(3, 0, 4))
+        TW = R(TAB, 0, 2048)
+
+        def gone(l, k, a, b):
+            o, i = R("G", 1024 * l + a, 1024 * l + b), IND(TW, R("OG", 64 * l + a // 16, 64 * l + b // 16))
+            if GS[k][l] == "v":
+                cp(o, i)
+            else:
+                act(o, i)
+        for l in range(4):
+            gone(l, 0, 0, 128)
+        mm(P(5, 0, 2), ID, R("NAT", 0, 128), True, False)
+        for l in range(4):
+            mm(P(5, 0, 2), sel("DA", 0, 8 + l), R("G", 1024 * l, 1024 * l + 128), False, l == 3)
+        act(R(PL, e3, e3 + 128), P(5, 0, 2))
+        send(PL, 1024, 256)
+        for h, (a, b) in enumerate(halves):
+            mm(P(h, 0, 7), ID, R("NAT", a, b), True, False)
+        for l in (0, 2, 1, 3):
+            gone(l, 1, 128, 576)
+            gone(l, 2, 576, 1024)
+            to_list(P(4, l), "DT", 0, "G", 1024 * l, 1024 * l + 1024)
+            for h, (a, b) in enumerate(halves):
+                mm(P(h, 0, 7), sel("DA", 0, 8 + l), R("G", 1024 * l + a, 1024 * l + b), False, l == 3)
+        for h, (a, b) in enumerate(halves):
+            act(R(PL, a, b), P(h, 0, 7))
+        tt(U("X", 0, 4), P(4, 0, 4), U("SP", 0, 4), A.add)
+        tt(U("SM", 0, 2), U("X", 0, 2), U("X", 2, 4), A.max)
+        tt(U("SM", 2), U("SM", 0), U("SM", 1), A.max)
+        tt(U("SM", 3), U("SM", 2), U("NL", 0), A.subtract)
+        ts(U("SI", 0), U("SM", 3), 0.0, A.max)
+        ts(U("SI", 1), U("SI", 0), 2, A.arith_shift_right, 7168, A.bitwise_and)
+        ts(U("SI", 2), U("SI", 0), 2047, A.bitwise_and)
+        tt(U("SM", 4), U("SI", 1), U("V4", 0), A.add)
+        cp(R("OS", 0, 64), U("SM", 4))
+        act(R("WS", 0, 1024), IND(R(PL, 3072, 8192), R("OS", 0, 64)))
+        ts(U("SI", 3), U("SI", 2), -1024.0, A.add, 0.0, A.max)
+        ts(U("SI", 4), U("SI", 3), 896, A.bitwise_and)
+        cp(R("OD", 0, 64), U("SI", 2))
+        ts(U("SI", 5), U("SI", 0), 16, A.arith_shift_right, 63, A.bitwise_and)
+        tt(U("SM", 5), U("SI", 2), U("SI", 4), A.add)
+        cp(R("OI", 0, 64), U("SM", 5))
+        act(R("IG", 0, 1024), IND(R(PL, 0, 3072), R("OI", 0, 64)))
+        ts(U("SM", 6), U("SI", 4), 2.0, A.mult, 127.0 - 3072.0, A.add)
+        ts(U("SM", 7), U("SI", 2), 1024.0, A.is_ge)
+        tt(U("SM", 8), U("SI", 5), U("SI", 2), A.subtract)
+        tt(U("SM", 10), U("SM", 6), U("SM", 8), A.add)
+        tt(U("SM", 11), U("SM", 10), U("SM", 7), A.mult)
+        ts(U("SM", 12), U("SI", 2), 3072.0, A.add)
+        ts(U("SM", 13), U("SM", 7), -992.0, A.mult, 1024.0, A.add)
+        tt(U("PT", 0), U("SM", 11), U("SM", 12), A.add)
+        ts(U("SM", 14), U("SM", 13), 2.0, A.mult)
+        tt(U("PT", 1), U("PT", 0), U("SM", 13), A.add)
+        cp(R("OW", 0, 128), U("PT", 0, 2))
+        tt(U("PT", 2), U("PT", 0), U("SM", 14), A.add)
+        tt(U("PT", 3), U("PT", 1), U("SM", 14), A.add)
+        cp(R("OW", 128, 256), U("PT", 2, 4))
+        ts(U("SM", 9), U("SI", 4), float(128 * me), A.not_equal, 1024.0, A.mult)
+        tt(U("SB", 1), U("SM", 9), U("SM", 7), A.mult)
+        ts(U("SB", 2), U("SM", 3), 0.0, A.is_ge, 2.0 ** -8, A.add)
+        act(U("SB", 3), U("SM", 3), F.Relu, scale=-1.0)
+        act(U("F2", 0, 4), U("X", 0, 4), F.Relu, bias=1.0)
+        tt(R("NE", 0, 1024), IND(R(H, 0, 2048), R("OD", 0, 64)), R("WS", 0, 1024), A.subtract)
+        for l in range(4):
+            mm(P(4, l), KP, U("SB", 2), True, False)
+            mm(P(4, l), eye("I4"), U("CB", l), False, True)
+            mm(P(5, 4 + l), ID, U("SB", 1))
+        mm(P(7, 0, 4), ID, U("P1", 0, 4), True, False)
+        mm(P(7, 0, 4), ID, U("P2", 0, 4), False, True)
+        tt(P(4, 4, 8), P(4, 0, 4), U("AI", 0, 4), A.add)
+        tt(U("FILL", 0, 4), P(4, 4, 8), U("EMP", 0, 4), A.min)
+        for h in range(2):
+            mm(P(h, 0, 8), ID, R("WS", 512 * h, 512 * h + 512), True, False)
+            mm(P(h, 0, 8), IN, R(HO, 512 * h, 512 * h + 512), False, True)
+            ts(R("Q", 512 * h, 512 * h + 512), P(h, 0, 8), 0.0, A.max, 255.5, A.add)
+            mm(P(h, 0, 8), ID, R(HO, 512 * h, 512 * h + 512), True, False)
+            mm(P(h, 0, 8), eye("IH"), R("Q", 512 * h, 512 * h + 512), False, True)
+            act(R(HN, 512 * h, 512 * h + 512), P(h, 0, 8), bias=-128.0)
+        if last:
+            dma("y", X(T.yh[:]), R(HN, 0, 1024))
+        else:
+            send(HX, 1024, 128, R(HN, 0, 128))
+            dma("y", R(HX, 0, 1024), R(HN, 0, 1024))
+            dma("y", R(HX, own0, own0 + 128), R(HN, 0, 128))
+        for l in range(4):
+            to_list(P(5, l), "DR", 144 * l, "IG", 0, 1024)
+        cp(U("RI", 0, 4), P(5, 0, 4))
+        ts(U("NM", 0, 4), U("RI", 0, 4), 2047, A.bitwise_and)
+        tt(U("V3", 0, 4), P(5, 4, 8), U("NM", 0, 4), A.is_le)
+        act(U("F2", 4, 8), P(5, 0, 4), F.Relu, scale=-1.0, bias=16384.0)
+        tt(P(7, 4, 8), U("NM", 0, 4), U("V3", 0, 4), A.mult)
+        cp(U("N8", 4, 8), P(7, 4, 8))
+        tt(U("FL", 4, 8), P(7, 4, 8), U("ME", 0, 4), A.is_equal)
+        cp(U("P1", 4, 8), P(7, 4, 8))
+        tt(U("P2", 4, 8), P(7, 4, 8), U("P1", 4, 8), A.subtract)
+        mm(P(6, 0, 8), eye("HP"), U("CC", 0, 8), True, False)
+        for k in range(8):
+            mm(P(6, k), KN, U("SB", 3), False, False)
+        mm(P(6, 0, 8), KN, U("F2", 0, 8), False, False)
+        mm(P(6, 4, 8), KP, U("V3", 0, 4), False, False)
+        mm(P(6, 0, 8), KN, U("FL", 0, 8), False, False)
+        mm(P(6, 0, 8), KN, U("P1", 0, 8), False, False)
+        mm(P(6, 0, 8), KN, U("P2", 0, 8), False, False)
+        for d in range(1, 8):
+            tt(U("O1", off[d - 1], off[d]), P(7, 0, 8 - d), U("N8", d, 8), A.subtract)
+        for a, b in SG:
+            act(U("O4", off[a], off[b]), U("O1", off[a], off[b]), F.Sign, bias=-0.5)
+            act(U("O2", off[a], off[b]), U("O1", off[a], off[b]), F.Sign, bias=0.5)
+        for d in range(1, 8):
+            mm(P(6, d, 8), eye("HP"), U("O4", off[d - 1], off[d]), False, False)
+            mm(P(6, 0, 8 - d), eye("HM"), U("O2", off[d - 1], off[d]), False, False)
+        mm(P(5, 0, 8), eye("IC"), U("CB", 0, 8), True, False)
+        mm(P(5, 0, 8), ID, U("P1", 0, 8), False, False)
+        mm(P(5, 0, 8), ID, U("P2", 0, 8), False, False)
+        PWIN = R(PL, 1024, 8192)
+        bank = 0
+        for l in range(4):
+            a = 8192 + 1024 * l
+            wd, src = R("WD", 1024 * l, 1024 * l + 1024), IND(PWIN, R("OW", 64 * l, 64 * l + 64))
+            if MODE[l] == "f":
+                tt(wd, src, R("NE", 0, 1024), A.subtract)
+                ts(R(PL, a, a + 1024), wd, 0.0, A.max, 255.0, A.min)
+            else:
+                act(wd, src)
+                for h in range(2):
+                    c = R("WD", 1024 * l + 512 * h, 1024 * l + 512 * h + 512)
+                    mm(P(bank, 0, 8), ID, c, True, False)
+                    mm(P(bank, 0, 8), IN, R("NE", 512 * h, 512 * h + 512), False, True)
+                    if MODE[l] == "s":
+                        act(c, P(bank, 0, 8), F.Relu)
+                    else:
+                        ts(R(PL, a + 512 * h, a + 512 * h + 512), P(bank, 0, 8), 0.0, A.max, 255.0, A.min)
+                    bank = (bank + 1) % 3
+                if MODE[l] == "s":
+                    ts(R(PL, a, a + 1024), wd, 255.0, A.min)
+            sums(4 + l, PL, a)
+        cp(U("Z", 4, 8), P(3, 4, 8))
+        for d in range(1, 8):
+            tt(U("O3", off[d - 1], off[d]), P(3, 0, 8 - d), U("Z", d, 8), A.is_ge)
+            mm(P(6, d, 8), KN, U("O3", off[d - 1], off[d]), False, False)
+            mm(P(6, 0, 8 - d), KP, U("O3", off[d - 1], off[d]), False, d == 7)
+        tt(U("KS", 0, 8), P(6, 0, 8), U("Z", 0, 8), A.add)
+        tt(P(4, 0, 8), P(6, 0, 8), U("Z", 0, 8), A.add)
+        act(U("KF", 0, 8), U("KS", 0, 8), F.Relu, scale=-1.0)
+        mm(P(5, 0, 8), IN, U("KF", 0, 8), False, False)
+        for d in range(1, 8):
+            tt(U("O1", off[d - 1], off[d]), P(4, 0, 8 - d), U("KS", d, 8), A.is_ge)
+            mm(P(5, d, 8), eye("RN"), U("O1", off[d - 1], off[d]), False, False)
+            mm(P(5, 0, 8 - d), eye("RP"), U("O1", off[d - 1], off[d]), False, d == 7)
+        for k in range(4):
+            act(P(k, 0, 4), P(5, 0, 4), F.Abs, bias=RK * (k - 8))
+            act(U("AS", 4 * k, 4 * k + 4), P(5, 4, 8), F.Abs, bias=RK * (k - 8))
+            tt(P(6, 2 * k, 2 * k + 2), P(k, 0, 2), U("AS", 4 * k, 4 * k + 2), A.min)
+            tt(U("L1", 2 * k, 2 * k + 2), P(k, 2, 4), U("AS", 4 * k + 2, 4 * k + 4), A.min)
+        tt(P(7, 0, 4), P(6, 0, 8, 2), U("L1", 0, 8, 2), A.min)
+        tt(U("L2", 0, 4), P(6, 1, 8, 2), U("L1", 1, 8, 2), A.min)
+        tt(P(7, 4, 8), P(7, 0, 4), U("FILL", 0, 4), A.min)
+        tt(U("S16", 0, 4), P(7, 4, 8), U("L2", 0, 4), A.min)
+        if not last:
+            ts(U("AI", 0, 4), U("S16", 0, 4), 4095, A.bitwise_and)
+            cp(R("OA", 0, 256), U("AI", 0, 4))
+        ts(U("T4", 0, 4), U("S16", 0, 4), 2, A.arith_shift_right, 15360, A.bitwise_and)
+        tt(U("PT", 0, 4), U("T4", 0, 4), U("V4", 0, 4), A.add)
+        cp(R("OP", 0, 256), U("PT", 0, 4))
+        ts(U("N8", 0, 4), U("S16", 0, 4), 2047, A.bitwise_and)
+        for l in range(4):
+            for a in (1024 * l, 1024 * l + 512):
+                o, i = R(PX, 4096 + a, 4608 + a), IND(R(PL, 3072, 12288), R("OP", a // 16, a // 16 + 32))
+                if last and l % 2:
+                    cp(o, i)
+                else:
+                    act(o, i)
+            if last:
+                dma("y", X(T.yw[:, 1024 * l:1024 * l + 1024]), R(PX, 4096 + 1024 * l, 5120 + 1024 * l))
+    ts(U("T4", 0, 4), U("N8", 0, 4), -1024.0, A.add, 0.0, A.max)
+    ts(P(0, 0, 4), U("N8", 0, 4), 1024.0, A.is_ge, float(-1024 - 1024 * me), A.mult)
+    ts(U("U4", 0, 4), U("T4", 0, 4), 896, A.bitwise_and)
+    tt(U("X", 0, 4), P(0, 0, 4), U("N8", 0, 4), A.add)
+    ts(P(0, 4, 8), U("U4", 0, 4), 7.0, A.mult, float(1024 * me), A.add)
+    tt(R("YN", 0, 256), P(0, 4, 8), U("X", 0, 4), A.add)
+    dma("y", X(T.yn[:]), R("YN", 0, 256))
+    return ops
+
+
+def links(ops):
+    hist = {}
+    lastq = {}
+    deps, soft = [], []
+    for i, o in enumerate(ops):
+        need, keepo = set(), set()
+        for w, fps in ((False, o["rd"]), (True, o["wr"])):
+            for (n, lo, hi, m, c) in fps:
+                ps = n.startswith("pb")
+                keep = []
+                if ps and hist.get(n) and hist[n][0][0] != i and ops[hist[n][0][0]]["q"] == o["q"]:
+                    keepo.add(hist[n][0][0])
+                for x in hist.get(n, []):
+                    j, jw, jlo, jhi, jm, jc = x
+                    hit = jlo < hi and lo < jhi and not (m == jm and c != jc)
+                    same = ops[j]["q"] == o["q"]
+                    if j != i:
+                        if ps and same and o["q"] == "t":
+                            keepo.add(j)
+                        elif (hit and (w or jw)) or (ps and not same):
+                            need.add(j)
+                    if ps:
+                        if same and o["q"] != "t":
+                            keep.append(x)
+                    elif not (w and m == 1 and lo <= jlo and jhi <= hi):
+                        keep.append(x)
+                keep.append((i, w, lo, hi, m, c))
+                hist[n] = keep
+        if o["q"] in ("g", "y"):
+            if o["q"] in lastq:
+                keepo.add(lastq[o["q"]])
+            lastq[o["q"]] = i
+        if o["kind"] == "a":
+            need, keepo = set(), {o["ns"]}
+        deps.append(need)
+        soft.append(keepo)
+    return deps, soft
+
+
+def arrange(ops, deps, soft):
+    n = len(ops)
+    hold = [0.0 if o["kind"] == "a" else (300.0 if o["kind"] == "r" else (60.0 if o["kind"] == "d" else o["ns"])) for o in ops]
+    done = [0.0 if o["kind"] == "a" else o["ns"] for o in ops]
+    succ = [[] for _ in ops]
+    left = [0] * n
+    for i in range(n):
+        for j in deps[i] | soft[i]:
+            succ[j].append(i)
+            left[i] += 1
+
+    def lag(j, i):
+        return done[j] + 60.0 if (j in deps[i] or ops[i]["kind"] == "a") else hold[j]
+    way = [0.0] * n
+    for j in range(n - 1, -1, -1):
+        way[j] = max([done[j]] + [lag(j, i) + way[i] for i in succ[j]]) + BONUS.get(ops[j]["wr"][0][0] if ops[j]["wr"] else "", 0)
+    can = [0.0] * n
+    ready = {}
+    free = {}
+    for i in range(n):
+        if not left[i]:
+            ready.setdefault(ops[i]["q"], []).append(i)
+    order = []
+    while len(order) < n:
+        best = None
+        for q, l in ready.items():
+            if l:
+                t = max(free.get(q, 0.0), min(can[i] for i in l))
+                if best is None or t < best[0]:
+                    best = (t, q)
+        t, q = best
+        i = max((i for i in ready[q] if can[i] <= t + 40.0), key=lambda i: (way[i], -i))
+        t = max(t, can[i])
+        ready[q].remove(i)
+        order.append(i)
+        free[q] = t + hold[i]
+        for k in succ[i]:
+            can[k] = max(can[k], t + lag(i, k))
+            left[k] -= 1
+            if not left[k]:
+                ready.setdefault(ops[k]["q"], []).append(k)
+    return order
+
+
+def emit(g, T, ops):
+    eng = {"v": g.vector, "s": g.scalar, "t": g.tensor, "g": g, "y": g.sync}
+    deps, soft = links(ops)
+    seq = arrange(ops, deps, soft)
+    order, cnt, place = {}, {}, {}
+    for n, i in enumerate(seq):
+        place[i] = n
+        if ops[i]["kind"] == "c":
+            cnt[ops[i]["q"]] = cnt.get(ops[i]["q"], 0) + 1
+            order[i] = cnt[ops[i]["q"]]
+    known = {q: {} for q in eng}
+    after, waits, used = {}, {}, set()
+    for i in seq:
+        o = ops[i]
+        if o["kind"] == "a":
+            continue
+        kn = known[o["q"]]
+        want = {}
+        for j in deps[i]:
+            p = ops[j]
+            if p["kind"] == "c":
+                key, v = p["q"], order[j]
+            elif p["kind"] == "w":
+                continue
+            else:
+                key, v = ("x", j), 1
+            if want.get(key, (0, 0))[0] < v:
+                want[key] = (v, j)
+        ws = []
+        for key, (v, j) in sorted(want.items(), key=lambda t: -place[t[1][1]]):
+            if kn.get(key, 0) >= v:
+                continue
+            ws.append(j)
+            used.add(j)
+            kn[key] = v
+            for k2, v2 in after.get(j, {}).items():
+                if kn.get(k2, 0) < v2:
+                    kn[k2] = v2
+        waits[i] = ws
+        after[i] = dict(kn)
+    tick, token = {}, {}
+    for i in seq:
+        o = ops[i]
+        if o["kind"] == "c" and i in used:
+            tick[o["q"]] = tick.get(o["q"], 0) + 1
+            token[i] = ("q" + o["q"], tick[o["q"]])
+        elif o["kind"] == "d":
+            token[i] = (o["extra"], 16)
+        elif o["kind"] in ("a", "r"):
+            token[i] = o["extra"]
+    sent = []
+    for i in seq:
+        o = ops[i]
+        if o["kind"] == "a":
+            continue
+        e = eng[o["q"]]
+        for j in waits[i]:
+            e.wait_ge(T.sem[token[j][0]], token[j][1])
+        if o["kind"] == "r":
+            while len(sent) > 2:
+                t = sent.pop(0)
+                e.wait_ge(T.sem[t[0]], t[1])
+            sent.append(token[i])
+        if o["fn"] is None:
+            continue
+        ins = o["fn"](e)
+        if o["kind"] == "d":
+            ins.then_inc(T.sem[token[i][0]], 16)
+        elif o["kind"] == "c" and i in used:
+            ins.then_inc(T.sem[token[i][0]], 1)
+    for i in seq:
+        if ops[i]["kind"] in ("d", "a", "r"):
+            g.wait_ge(T.sem[token[i][0]], token[i][1])
+    for q in tick:
+        g.wait_ge(T.sem["q" + q], tick[q])
+
+
+def rank_program(g, core, T, topo):
+    if T.rank_of(core) is None:
+        return
+    emit(g, T, build(T, topo, core))

@@ -6,12 +6,16 @@ F = ActivationFunctionType
 RO = 3
 BIG = float(2 ** 25)
 RK = float(2 ** 19)
-MODE = "bbbb"
-ASR = ("vvss", "vvvv", "vvvv")
+MODE = "fbbb"
+ASR = ("vvss", "vvvs", "vvvs")
 GS = ("vvvv", "vvss", "vvss")
-TB = "vs"
 SG = ((0, 1), (1, 3), (3, 7))
-BONUS = {"OP": 6000, "OG": 3000, "NAT": 2000}
+TRIES = 1500
+BONUS = {'vOP': 4000, 'sNAT': 1750, 'vX': 600, 'sIH': 350, 'sIN': -600, 'vD': 4500, 'vTAB1': 900, 'sTAB2': 1500, 'sKP': 500,
+         'vFILL': -250, 'vWB': 850, 'vPA': -600, 'vCOL': -600, 'sHN': -1500, 'sJUNK': 3000, 'vTAB0': 250, 'vOD': 250, 'sME': 1500,
+         'spb1': 600, 'sWP': 1500, 'vQ': 1500, 'sCMP': 600, 'sF2': 1750, 'sG': -250, 'sKF': -600, 'sWD': -1200, 'sWS': 250,
+         'vL2': 250, 'sTAB1': 1500, 'vNE': -1500, 'sHM': -1500, 'sDA': -1500}
+PLAN = {}
 
 SCRATCH = {}
 
@@ -28,13 +32,13 @@ for _i in range(8):
     SCRATCH["pb%d" % _i] = ("psum", [128, 8, 64], "float32")
 for _i in range(RO):
     _sb("H%d" % _i, 4096, "bfloat16")
-    _sb("TAB%d" % _i, 2048, "bfloat16")
+    _sb("TAB%d" % _i, 4096, "bfloat16")
 for _i in range(RO + 1):
     _sb("HO%d" % _i, 1024, "bfloat16")
 for _n, _w in (("PL0", 12288), ("PL1", 12288), ("CMP", 4096), ("G", 4096), ("WD", 4096), ("NAT", 1024), ("IG", 1024), ("WS", 1024),
                ("NE", 1024), ("Q", 1024), ("FB", 128), ("JUNK", 128), ("DN", 144), ("DT", 144), ("DS", 144), ("DA", 144), ("DR", 576),
                ("WP", 2304), ("BL", 128), ("ID", 128), ("IN", 128), ("IH", 128), ("KP", 128), ("KN", 128), ("RP", 128), ("RN", 128),
-               ("I4", 128), ("IC", 128), ("D", 144), ("DH", 144), ("HP", 128), ("HM", 128), ("HN", 1792)):
+               ("I4", 128), ("IC", 128), ("D", 144), ("DH", 144), ("HP", 128), ("HM", 128), ("HN", 1792), ("WB", 528)):
     _sb(_n, _w, "bfloat16")
 for _n, _w in (("J", 144), ("JG", 128), ("JR", 128), ("COL", 32), ("EQ", 16), ("WR", 16), ("C8", 4), ("WOULD", 128), ("CUM", 128),
                ("PA", 128), ("DB", 128), ("ONE", 128), ("ACC", 8)):
@@ -42,18 +46,18 @@ for _n, _w in (("J", 144), ("JG", 128), ("JR", 128), ("COL", 32), ("EQ", 16), ("
 _sb("KC", 8, "int32")
 _sb("NB", 256, "int32")
 _sb("YN", 256, "float32")
-for _n, _w in (("OA", 256), ("OG", 256), ("OP", 256), ("OW", 256), ("OS", 64), ("OD", 64), ("OI", 64), ("OC", 8)):
+for _n, _w in (("OA", 256), ("OP", 256), ("OW", 256), ("OS", 64), ("OD", 64), ("OI", 64), ("OC", 8)):
     _sb(_n, _w, "uint16")
-for _n, _u in (("N8", 8), ("S16", 4), ("AI", 4), ("RI", 4), ("NM", 4), ("T4", 4), ("U4", 4), ("W4", 4), ("SI", 8), ("VI", 4), ("PRI", 4)):
+for _n, _u in (("N8", 8), ("S16", 4), ("RI", 4), ("NM", 4), ("T4", 4), ("U4", 4), ("W4", 4), ("SI", 8), ("VI", 4), ("PRI", 4)):
     _su(_n, _u, "int32")
 for _n, _u in (("KS", 8), ("Z", 8), ("SP", 4), ("X", 4), ("SM", 16), ("ME", 4), ("V4", 4), ("EMP", 4), ("FILL", 4),
-               ("AS", 16), ("L1", 8), ("L2", 4), ("NL", 1), ("PT", 4)):
+               ("AS", 16), ("L1", 8), ("L2", 4), ("PT", 4)):
     _su(_n, _u, "float32")
 for _n, _u in (("P1", 8), ("P2", 8), ("FL", 8), ("F2", 8), ("V3", 4), ("SB", 4), ("CB", 8), ("CC", 8), ("KF", 8), ("O1", 28), ("O2", 28),
-               ("O3", 28), ("O4", 28)):
+               ("O3", 28), ("O4", 28), ("NL", 2)):
     _su(_n, _u, "bfloat16")
 
-SEMAPHORES = ["qv", "qs", "qt", "qg"] + ["d%d" % _i for _i in range(24)]
+SEMAPHORES = ["qv", "qs", "qt", "qg"] + ["d%d" % _i for _i in range(32)]
 for _i in range(3 * RO):
     SEMAPHORES += ["xa%d" % _i, "xb%d" % _i, "xl%d" % _i, "xf%d" % _i]
 
@@ -61,6 +65,7 @@ for _i in range(3 * RO):
 def build(T, topo, core):
     me = T.rank_of(core)
     ops = []
+    phase = [0]
 
     def R(n, lo, hi, st=1):
         return (T[n][:, lo:hi:st] if st > 1 else T[n][:, lo:hi], [(n, lo, hi, st, lo % st)], (hi - lo + st - 1) // st, n)
@@ -93,7 +98,7 @@ def build(T, topo, core):
         return 60 + 1.04 * max(64, k * a[2])
 
     def add(q, fn, rd, wr, ns, kind="c", extra=None):
-        ops.append({"q": q, "fn": fn, "rd": rd, "wr": wr, "ns": ns, "kind": kind, "extra": extra})
+        ops.append({"q": q, "fn": fn, "rd": rd, "wr": wr, "ns": ns, "kind": kind, "extra": extra, "at": phase[0]})
 
     def tt(o, a, b, op):
         k = 1.0 if (str(a[3]).startswith("pb") or b[3].startswith("pb")) else 2.0
@@ -187,9 +192,9 @@ def build(T, topo, core):
     def every16(src, lo, hi, p):
         return (T[src][:, lo + p:hi:16], [(src, lo, hi, 1, 0)], (hi - lo) // 16, src)
 
-    def to_list(o, n, base, src, lo, hi):
+    def to_list(o, n, base, src, lo, hi, first=True):
         for p in range(16):
-            mm(o, sel(n, base, p), every16(src, lo, hi, p), p == 0, p == 15)
+            mm(o, sel(n, base, p), every16(src, lo, hi, p), first and p == 0, p == 15)
 
     def col(i):
         return R("COL", i, i + 1)
@@ -244,11 +249,11 @@ def build(T, topo, core):
     ts(P(1, 0, 4), U("V4", 0, 4), 128.0, A.is_lt, float(own0), A.mult)
     tt(P(0, 4, 8), P(0, 0, 4), U("W4", 0, 4), A.mult)
     tt(P(1, 4, 8), P(1, 0, 4), U("V4", 0, 4), A.add)
-    tt(U("N8", 0, 4), P(0, 4, 8), U("U4", 0, 4), A.add)
-    tt(U("T4", 0, 4), P(1, 4, 8), U("N8", 0, 4), A.is_equal)
+    tt(U("NM", 0, 4), P(0, 4, 8), U("U4", 0, 4), A.add)
+    tt(U("T4", 0, 4), P(1, 4, 8), U("NM", 0, 4), A.is_equal)
     ts(P(0, 0, 4), U("T4", 0, 4), 2048.0, A.mult)
-    tt(U("AI", 0, 4), P(0, 0, 4), U("N8", 0, 4), A.add)
-    cp(R("OA", 0, 256), U("AI", 0, 4))
+    tt(U("N8", 0, 4), P(0, 0, 4), U("NM", 0, 4), A.add)
+    cp(R("OA", 0, 256), U("N8", 0, 4))
     act(U("ME", 0, 4), P(1, 4, 8))
     act(U("EMP", 0, 4), P(1, 4, 8), bias=2048.0 + 2 ** 17 + 2 ** 16)
     ts(R("PA", 0, 128), R("JR", 0, 128), 4.0, A.is_equal)
@@ -266,10 +271,12 @@ def build(T, topo, core):
     ts(col(11), R("EQ", 4, 5), 65536.0, A.mult)
     ts(col(12), col(4), -2.0 * BIG, A.mult, col(11), A.add)
     ts(R("WR", 8, 12), R("EQ", 8, 12), 16384.0, A.mult)
-    ts(R("C8", 0, 4), R("J", 0, 4), 2048.0, A.mult, 128.0, A.add)
+    ts(R("C8", 0, 4), R("J", 0, 4), 256.0, A.mult, 128.0, A.add)
     tt(R("WR", 4, 8), R("EQ", 4, 8), R("EQ", 0, 4), A.add)
     ts(U("PRI", 0, 4), U("PRI", 0, 4), float(4096 - 2 ** 22), A.mult, float(3 * 2 ** 22 + 4096 + 32 * 65536), A.add)
     tt(R("WR", 0, 4), R("WR", 4, 8), R("WR", 8, 12), A.add)
+    ms(R("TAB0", 2048, 4096), 1.0)
+    ms(R("WB", 512, 528), 0.0)
     ms(R("PL0", 0, 128), 0.0)
     ms(R("PL1", 0, 128), 0.0)
     ms(R("PL0", 3072, 4096), 0.0)
@@ -286,6 +293,8 @@ def build(T, topo, core):
         act(eye(n), eye("ID"), scale=s)
     add("y", None, fp(R("H0", 1024, 2048)), [], 0, "w")
     dma("y", R("PL0", 4096, 8192), X(T.w0[:]), 6000)
+    dma("y", R("TAB1", 2048, 4096), R("TAB0", 2048, 4096))
+    dma("y", R("TAB2", 2048, 4096), R("TAB0", 2048, 4096))
     dma("y", R("H1", 2048, 4096), R("H0", 2048, 4096))
     dma("y", R("H2", 2048, 4096), R("H0", 2048, 4096))
     dma("y", R("PL1", 3072, 4096), R("PL0", 3072, 4096))
@@ -294,10 +303,6 @@ def build(T, topo, core):
     off = [0]
     for d in range(1, 8):
         off.append(off[-1] + 8 - d)
-
-    def pieces(a):
-        cp(U("P1", a, a + 4), U("N8", a, a + 4))
-        tt(U("P2", a, a + 4), U("N8", a, a + 4), U("P1", a, a + 4), A.subtract)
 
     def sums(c, src, lo):
         for p in range(16):
@@ -311,6 +316,7 @@ def build(T, topo, core):
         HW = R(H, 0, 4096)
         last = r == RO - 1
         ASL = ASR[r]
+        phase[0] = 4 * r + 1
         for l in range(4):
             tt(R("CMP", 1024 * l, 1024 * l + 128), IND(HW, R("OA", 64 * l, 64 * l + 8)), R(HO, 0, 128), A.is_lt)
         for l in range(4):
@@ -322,14 +328,15 @@ def build(T, topo, core):
             fp(R("ONE", 0, 128), R("WOULD", 0, 128)), fp(R("CUM", 0, 128)), 200)
         tt(R(TAB, own0, own0 + 128), R("CUM", 0, 128), P(4, 2, 4), A.max)
         send(TAB, 1024, 128)
-        cp(R("OG", 0, 256), U("N8", 0, 4))
-        pieces(0)
+        cp(U("P1", 0, 4), U("N8", 0, 4))
+        tt(U("P2", 0, 4), U("N8", 0, 4), U("P1", 0, 4), A.subtract)
         for h in range(2):
             for p in range(8 * h, 8 * h + 8):
                 for f in range(8):
                     mm(P(6 + h, p % 8), sel("WP", 144 * p, f), U("P%d" % (1 + f // 4), f % 4), f == 0, f == 7)
             for p in range(8 * h, 8 * h + 8):
                 act(R("NAT", p, 1024, 16), P(6 + h, p % 8))
+        phase[0] = 4 * r + 2
         seq = [l for l in range(4) if ASL[l] == "v"]
         seq = seq[:-1] + [l for l in range(4) if ASL[l] == "s"] + seq[-1:]
         for h, (a, b) in enumerate(halves):
@@ -352,25 +359,24 @@ def build(T, topo, core):
         if not last:
             ts(R("PA", 0, 128), R(TAB, own0, own0 + 128), -1.0, A.add, 1000.0, A.mult)
             tt(R("DB", 0, 128), R("PA", 0, 128), R("DB", 0, 128), A.min)
-        for h, (a, b) in enumerate(halves):
-            if TB[h] == "v":
-                ts(R(TAB, a, b), P(h, 0, 7), bias[r], A.add, 0.0, A.max)
-            else:
-                act(R(TAB, a, b), P(h, 0, 7), F.Relu, bias=bias[r])
+        ts(R(TAB, 128, 576), P(0, 0, 7), bias[r], A.add, 0.0, A.max)
+        act(R(TAB, 576, 1024), P(1, 0, 7), F.Relu, bias=bias[r])
         e3 = 1024 + 256 * me
-        act(R(PL, e3 + 128, e3 + 256), IND(R(PL, 4096, 8192), R("OC", 0, 8)))
+        if r == 0:
+            for l in range(4):
+                act(R("WB", 128 * l, 128 * l + 128), R(PL, 4096 + 1024 * l, 4224 + 1024 * l))
+        act(R(PL, e3 + 128, e3 + 256), IND(R("WB", 0, 528), R("OC", 0, 8)))
         to_list(P(4, 4), "DT", 0, TAB, 0, 1024)
         tt(U("SP", 0, 4), U("N8", 0, 4), U("PRI", 0, 4), A.add)
-        ts(U("FL", 0, 4), U("AI", 0, 4), 2048.0, A.is_ge)
-        ts(U("SM", 15), P(4, 4), -BIG, A.is_gt, BIG, A.mult)
-        tt(U("NL", 0), U("NL", 0), U("SM", 15), A.max)
+        ts(U("NL", 1), P(4, 4), -BIG, A.is_gt, BIG, A.mult)
+        tt(U("NL", 0), U("NL", 0), U("NL", 1), A.max)
         for l in range(4):
             sums(l, PL, 4096 + 1024 * l)
         act(U("Z", 0, 4), P(3, 0, 4))
-        TW = R(TAB, 0, 2048)
+        TW = R(TAB, 0, 4096)
 
         def gone(l, k, a, b):
-            o, i = R("G", 1024 * l + a, 1024 * l + b), IND(TW, R("OG", 64 * l + a // 16, 64 * l + b // 16))
+            o, i = R("G", 1024 * l + a, 1024 * l + b), IND(TW, R("OA", 64 * l + a // 16, 64 * l + b // 16))
             if GS[k][l] == "v":
                 cp(o, i)
             else:
@@ -382,20 +388,21 @@ def build(T, topo, core):
             mm(P(5, 0, 2), sel("DA", 0, 8 + l), R("G", 1024 * l, 1024 * l + 128), False, l == 3)
         act(R(PL, e3, e3 + 128), P(5, 0, 2))
         send(PL, 1024, 256)
+        phase[0] = 4 * r + 3
         for h, (a, b) in enumerate(halves):
             mm(P(h, 0, 7), ID, R("NAT", a, b), True, False)
         for l in (0, 2, 1, 3):
             gone(l, 1, 128, 576)
             gone(l, 2, 576, 1024)
-            to_list(P(4, l), "DT", 0, "G", 1024 * l, 1024 * l + 1024)
+            mm(P(4, l), IN, U("NL", 0), True, False)
+            to_list(P(4, l), "DT", 0, "G", 1024 * l, 1024 * l + 1024, False)
             for h, (a, b) in enumerate(halves):
                 mm(P(h, 0, 7), sel("DA", 0, 8 + l), R("G", 1024 * l + a, 1024 * l + b), False, l == 3)
         for h, (a, b) in enumerate(halves):
             act(R(PL, a, b), P(h, 0, 7))
         tt(U("X", 0, 4), P(4, 0, 4), U("SP", 0, 4), A.add)
         tt(U("SM", 0, 2), U("X", 0, 2), U("X", 2, 4), A.max)
-        tt(U("SM", 2), U("SM", 0), U("SM", 1), A.max)
-        tt(U("SM", 3), U("SM", 2), U("NL", 0), A.subtract)
+        tt(U("SM", 3), U("SM", 0), U("SM", 1), A.max)
         ts(U("SI", 0), U("SM", 3), 0.0, A.max)
         ts(U("SI", 1), U("SI", 0), 2, A.arith_shift_right, 7168, A.bitwise_and)
         ts(U("SI", 2), U("SI", 0), 2047, A.bitwise_and)
@@ -417,7 +424,7 @@ def build(T, topo, core):
         ts(U("SM", 12), U("SI", 2), 3072.0, A.add)
         ts(U("SM", 13), U("SM", 7), -992.0, A.mult, 1024.0, A.add)
         tt(U("PT", 0), U("SM", 11), U("SM", 12), A.add)
-        ts(U("SM", 14), U("SM", 13), 2.0, A.mult)
+        ts(U("SM", 14), U("SM", 7), -1984.0, A.mult, 2048.0, A.add)
         tt(U("PT", 1), U("PT", 0), U("SM", 13), A.add)
         cp(R("OW", 0, 128), U("PT", 0, 2))
         tt(U("PT", 2), U("PT", 0), U("SM", 14), A.add)
@@ -435,7 +442,7 @@ def build(T, topo, core):
             mm(P(5, 4 + l), ID, U("SB", 1))
         mm(P(7, 0, 4), ID, U("P1", 0, 4), True, False)
         mm(P(7, 0, 4), ID, U("P2", 0, 4), False, True)
-        tt(P(4, 4, 8), P(4, 0, 4), U("AI", 0, 4), A.add)
+        tt(P(4, 4, 8), P(4, 0, 4), U("N8", 0, 4), A.add)
         tt(U("FILL", 0, 4), P(4, 4, 8), U("EMP", 0, 4), A.min)
         for h in range(2):
             mm(P(h, 0, 8), ID, R("WS", 512 * h, 512 * h + 512), True, False)
@@ -450,10 +457,11 @@ def build(T, topo, core):
             send(HX, 1024, 128, R(HN, 0, 128))
             dma("y", R(HX, 0, 1024), R(HN, 0, 1024))
             dma("y", R(HX, own0, own0 + 128), R(HN, 0, 128))
+        phase[0] = 4 * r + 4
         for l in range(4):
             to_list(P(5, l), "DR", 144 * l, "IG", 0, 1024)
         cp(U("RI", 0, 4), P(5, 0, 4))
-        ts(U("NM", 0, 4), U("RI", 0, 4), 2047, A.bitwise_and)
+        ts(U("NM", 0, 4), U("RI", 0, 4), 4095, A.bitwise_and)
         tt(U("V3", 0, 4), P(5, 4, 8), U("NM", 0, 4), A.is_le)
         act(U("F2", 4, 8), P(5, 0, 4), F.Relu, scale=-1.0, bias=16384.0)
         tt(P(7, 4, 8), U("NM", 0, 4), U("V3", 0, 4), A.mult)
@@ -466,7 +474,9 @@ def build(T, topo, core):
             mm(P(6, k), KN, U("SB", 3), False, False)
         mm(P(6, 0, 8), KN, U("F2", 0, 8), False, False)
         mm(P(6, 4, 8), KP, U("V3", 0, 4), False, False)
-        mm(P(6, 0, 8), KN, U("FL", 0, 8), False, False)
+        act(U("KF", 0, 8), P(7, 0, 8), F.Relu, bias=-2047.0)
+        mm(P(6, 4, 8), KN, U("FL", 4, 8), False, False)
+        mm(P(6, 0, 8), KN, U("KF", 0, 8), False, False)
         mm(P(6, 0, 8), KN, U("P1", 0, 8), False, False)
         mm(P(6, 0, 8), KN, U("P2", 0, 8), False, False)
         for d in range(1, 8):
@@ -491,16 +501,10 @@ def build(T, topo, core):
             else:
                 act(wd, src)
                 for h in range(2):
-                    c = R("WD", 1024 * l + 512 * h, 1024 * l + 512 * h + 512)
-                    mm(P(bank, 0, 8), ID, c, True, False)
+                    mm(P(bank, 0, 8), ID, R("WD", 1024 * l + 512 * h, 1024 * l + 512 * h + 512), True, False)
                     mm(P(bank, 0, 8), IN, R("NE", 512 * h, 512 * h + 512), False, True)
-                    if MODE[l] == "s":
-                        act(c, P(bank, 0, 8), F.Relu)
-                    else:
-                        ts(R(PL, a + 512 * h, a + 512 * h + 512), P(bank, 0, 8), 0.0, A.max, 255.0, A.min)
+                    ts(R(PL, a + 512 * h, a + 512 * h + 512), P(bank, 0, 8), 0.0, A.max, 255.0, A.min)
                     bank = (bank + 1) % 3
-                if MODE[l] == "s":
-                    ts(R(PL, a, a + 1024), wd, 255.0, A.min)
             sums(4 + l, PL, a)
         cp(U("Z", 4, 8), P(3, 4, 8))
         for d in range(1, 8):
@@ -525,12 +529,16 @@ def build(T, topo, core):
         tt(P(7, 4, 8), P(7, 0, 4), U("FILL", 0, 4), A.min)
         tt(U("S16", 0, 4), P(7, 4, 8), U("L2", 0, 4), A.min)
         if not last:
-            ts(U("AI", 0, 4), U("S16", 0, 4), 4095, A.bitwise_and)
-            cp(R("OA", 0, 256), U("AI", 0, 4))
+            ts(U("N8", 0, 4), U("S16", 0, 4), 4095, A.bitwise_and)
+            cp(R("OA", 0, 256), U("N8", 0, 4))
         ts(U("T4", 0, 4), U("S16", 0, 4), 2, A.arith_shift_right, 15360, A.bitwise_and)
         tt(U("PT", 0, 4), U("T4", 0, 4), U("V4", 0, 4), A.add)
         cp(R("OP", 0, 256), U("PT", 0, 4))
-        ts(U("N8", 0, 4), U("S16", 0, 4), 2047, A.bitwise_and)
+        if last:
+            ts(U("N8", 0, 4), U("S16", 0, 4), 2047, A.bitwise_and)
+        else:
+            for l in range(4):
+                act(R("WB", 128 * l, 128 * l + 128), IND(R(PL, 3072, 12288), R("OP", 64 * l, 64 * l + 8)))
         for l in range(4):
             for a in (1024 * l, 1024 * l + 512):
                 o, i = R(PX, 4096 + a, 4608 + a), IND(R(PL, 3072, 12288), R("OP", a // 16, a // 16 + 32))
@@ -538,15 +546,16 @@ def build(T, topo, core):
                     cp(o, i)
                 else:
                     act(o, i)
-            if last:
-                dma("y", X(T.yw[:, 1024 * l:1024 * l + 1024]), R(PX, 4096 + 1024 * l, 5120 + 1024 * l))
+        if last:
+            for a in (0, 1024, 512, 1536, 2048, 3072, 2560, 3584):
+                dma("y", X(T.yw[:, a:a + 512]), R(PX, 4096 + a, 4608 + a))
     ts(U("T4", 0, 4), U("N8", 0, 4), -1024.0, A.add, 0.0, A.max)
     ts(P(0, 0, 4), U("N8", 0, 4), 1024.0, A.is_ge, float(-1024 - 1024 * me), A.mult)
     ts(U("U4", 0, 4), U("T4", 0, 4), 896, A.bitwise_and)
     tt(U("X", 0, 4), P(0, 0, 4), U("N8", 0, 4), A.add)
     ts(P(0, 4, 8), U("U4", 0, 4), 7.0, A.mult, float(1024 * me), A.add)
     tt(R("YN", 0, 256), P(0, 4, 8), U("X", 0, 4), A.add)
-    dma("y", X(T.yn[:]), R("YN", 0, 256))
+    dma("s", X(T.yn[:]), R("YN", 0, 256))
     return ops
 
 
@@ -589,7 +598,11 @@ def links(ops):
     return deps, soft
 
 
-def arrange(ops, deps, soft):
+def tag(o):
+    return (o["q"] + o["wr"][0][0], o["at"]) if o["wr"] and o["q"] else None
+
+
+def arrange(ops, deps, soft, bonus):
     n = len(ops)
     hold = [0.0 if o["kind"] == "a" else (300.0 if o["kind"] == "r" else (60.0 if o["kind"] == "d" else o["ns"])) for o in ops]
     done = [0.0 if o["kind"] == "a" else o["ns"] for o in ops]
@@ -597,14 +610,11 @@ def arrange(ops, deps, soft):
     left = [0] * n
     for i in range(n):
         for j in deps[i] | soft[i]:
-            succ[j].append(i)
+            succ[j].append((i, done[j] + 60.0 if (j in deps[i] or ops[i]["kind"] == "a") else hold[j]))
             left[i] += 1
-
-    def lag(j, i):
-        return done[j] + 60.0 if (j in deps[i] or ops[i]["kind"] == "a") else hold[j]
     way = [0.0] * n
     for j in range(n - 1, -1, -1):
-        way[j] = max([done[j]] + [lag(j, i) + way[i] for i in succ[j]]) + BONUS.get(ops[j]["wr"][0][0] if ops[j]["wr"] else "", 0)
+        way[j] = max([done[j]] + [lag + way[i] for i, lag in succ[j]]) + bonus.get(tag(ops[j]), 0)
     can = [0.0] * n
     ready = {}
     free = {}
@@ -625,18 +635,68 @@ def arrange(ops, deps, soft):
         ready[q].remove(i)
         order.append(i)
         free[q] = t + hold[i]
-        for k in succ[i]:
-            can[k] = max(can[k], t + lag(i, k))
+        for k, lag in succ[i]:
+            can[k] = max(can[k], t + lag)
             left[k] -= 1
             if not left[k]:
                 ready.setdefault(ops[k]["q"], []).append(k)
     return order
 
 
+def length(ops, deps, seq, gath, f, fg, hop):
+    end, free = {}, {}
+    for i in seq:
+        o = ops[i]
+        k = o["kind"]
+        if k == "a":
+            end[i] = end[o["ns"]]
+            continue
+        t = free.get(o["q"], 0.0)
+        for j in deps[i]:
+            if end[j] + 60.0 > t:
+                t = end[j] + 60.0
+        if k == "c":
+            d = o["ns"] * f if o["q"] == "t" else 60.0 + (o["ns"] - 60.0) * (fg if gath[i] else f)
+            free[o["q"]] = end[i] = t + d
+        elif k == "r":
+            free["g"], end[i] = t + 300.0, t + hop
+        elif k == "d":
+            free[o["q"]], end[i] = t + 50.0, t + o["ns"]
+        else:
+            free[o["q"]] = end[i] = t
+    return max(end.values())
+
+
+def plan(ops, deps, soft):
+    if "bonus" not in PLAN:
+        gath = [any(SCRATCH[x[0]][2] == "uint16" for x in o["rd"]) for o in ops]
+        keys = sorted({tag(o) for o in ops if o["wr"] and o["q"] in ("v", "s", "t")})
+
+        def cost(b):
+            seq = arrange(ops, deps, soft, b)
+            return (length(ops, deps, seq, gath, 0.8, 0.8, 2300.0) / 142 + length(ops, deps, seq, gath, 1.15, 1.55, 3600.0) / 212
+                    + length(ops, deps, seq, gath, 1.0, 0.75, 3000.0) / 160)
+        b = {k: BONUS.get(k[0], 0) for k in keys}
+        best = cost(b)
+        x = 12345
+        for _ in range(TRIES):
+            c = dict(b)
+            for _k in range(1 + (x >> 8) % 3):
+                x = (x * 1103515245 + 12345) % 2147483648
+                k = keys[(x >> 8) % len(keys)]
+                x = (x * 1103515245 + 12345) % 2147483648
+                c[k] += (-1500, -600, -250, 250, 600, 1500, 3000)[(x >> 8) % 7]
+            v = cost(c)
+            if v < best:
+                best, b = v, c
+        PLAN["bonus"] = b
+    return PLAN["bonus"]
+
+
 def emit(g, T, ops):
     eng = {"v": g.vector, "s": g.scalar, "t": g.tensor, "g": g, "y": g.sync}
     deps, soft = links(ops)
-    seq = arrange(ops, deps, soft)
+    seq = arrange(ops, deps, soft, plan(ops, deps, soft))
     order, cnt, place = {}, {}, {}
     for n, i in enumerate(seq):
         place[i] = n

from concourse.bass import DstId, RemoteDMATransfer
from concourse.mybir import AluOpType, ActivationFunctionType

A = AluOpType
F = ActivationFunctionType
RO = 3
BIG = float(2 ** 25)
RK = float(2 ** 19)
MODE = "fbbb"
ASR = ("vvss", "vvvs", "vvvs")
GS = ("vvvv", "vvss", "vvss")
SG = ((0, 1), (1, 3), (3, 7))
TRIES = 1500
BONUS = {'vOP': 4000, 'sNAT': 1750, 'vX': 600, 'sIH': 350, 'sIN': -600, 'vD': 4500, 'vTAB1': 900, 'sTAB2': 1500, 'sKP': 500,
         'vFILL': -250, 'vWB': 850, 'vPA': -600, 'vCOL': -600, 'sHN': -1500, 'sJUNK': 3000, 'vTAB0': 250, 'vOD': 250, 'sME': 1500,
         'spb1': 600, 'sWP': 1500, 'vQ': 1500, 'sCMP': 600, 'sF2': 1750, 'sG': -250, 'sKF': -600, 'sWD': -1200, 'sWS': 250,
         'vL2': 250, 'sTAB1': 1500, 'vNE': -1500, 'sHM': -1500, 'sDA': -1500}
PLAN = {}

SCRATCH = {}


def _sb(n, w, d):
    SCRATCH[n] = ("sbuf", [128, w], d)


def _su(n, u, d):
    SCRATCH[n] = ("sbuf", [128, u, 64], d)


for _i in range(8):
    SCRATCH["pb%d" % _i] = ("psum", [128, 8, 64], "float32")
for _i in range(RO):
    _sb("H%d" % _i, 4096, "bfloat16")
    _sb("TAB%d" % _i, 4096, "bfloat16")
for _i in range(RO + 1):
    _sb("HO%d" % _i, 1024, "bfloat16")
for _n, _w in (("PL0", 12288), ("PL1", 12288), ("CMP", 4096), ("G", 4096), ("WD", 4096), ("NAT", 1024), ("IG", 1024), ("WS", 1024),
               ("NE", 1024), ("Q", 1024), ("FB", 128), ("JUNK", 128), ("DN", 144), ("DT", 144), ("DS", 144), ("DA", 144), ("DR", 576),
               ("WP", 2304), ("BL", 128), ("ID", 128), ("IN", 128), ("IH", 128), ("KP", 128), ("KN", 128), ("RP", 128), ("RN", 128),
               ("I4", 128), ("IC", 128), ("D", 144), ("DH", 144), ("HP", 128), ("HM", 128), ("HN", 1792), ("WB", 528)):
    _sb(_n, _w, "bfloat16")
for _n, _w in (("J", 144), ("JG", 128), ("JR", 128), ("COL", 32), ("EQ", 16), ("WR", 16), ("C8", 4), ("WOULD", 128), ("CUM", 128),
               ("PA", 128), ("DB", 128), ("ONE", 128), ("ACC", 8)):
    _sb(_n, _w, "float32")
_sb("KC", 8, "int32")
_sb("NB", 256, "int32")
_sb("YN", 256, "float32")
for _n, _w in (("OA", 256), ("OP", 256), ("OW", 256), ("OS", 64), ("OD", 64), ("OI", 64), ("OC", 8)):
    _sb(_n, _w, "uint16")
for _n, _u in (("N8", 8), ("S16", 4), ("RI", 4), ("NM", 4), ("T4", 4), ("U4", 4), ("W4", 4), ("SI", 8), ("VI", 4), ("PRI", 4)):
    _su(_n, _u, "int32")
for _n, _u in (("KS", 8), ("Z", 8), ("SP", 4), ("X", 4), ("SM", 16), ("ME", 4), ("V4", 4), ("EMP", 4), ("FILL", 4),
               ("AS", 16), ("L1", 8), ("L2", 4), ("PT", 4)):
    _su(_n, _u, "float32")
for _n, _u in (("P1", 8), ("P2", 8), ("FL", 8), ("F2", 8), ("V3", 4), ("SB", 4), ("CB", 8), ("CC", 8), ("KF", 8), ("O1", 28), ("O2", 28),
               ("O3", 28), ("O4", 28), ("NL", 2)):
    _su(_n, _u, "bfloat16")

SEMAPHORES = ["qv", "qs", "qt", "qg"] + ["d%d" % _i for _i in range(32)]
for _i in range(3 * RO):
    SEMAPHORES += ["xa%d" % _i, "xb%d" % _i, "xl%d" % _i, "xf%d" % _i]


def build(T, topo, core):
    me = T.rank_of(core)
    ops = []
    phase = [0]

    def R(n, lo, hi, st=1):
        return (T[n][:, lo:hi:st] if st > 1 else T[n][:, lo:hi], [(n, lo, hi, st, lo % st)], (hi - lo + st - 1) // st, n)

    def U(n, a, b=None, st=1):
        b = a + 1 if b is None else b
        return (T[n][:, a:b:st, :] if st > 1 else T[n][:, a:b, :], [(n, 64 * a, 64 * b, st, a % st)], 64 * ((b - a + st - 1) // st), n)

    def P(bank, a, b=None, st=1):
        return U("pb%d" % bank, a, b, st)

    def IND(win, off):
        return (win[0].indirect(off[0]), win[1] + off[1], 16 * off[2], None)

    def fp(*xs):
        r = []
        for x in xs:
            if isinstance(x, tuple):
                r += x[1]
        return r

    def val(x):
        return x[0] if isinstance(x, tuple) else x

    def span(o, a, k=None):
        if a[3] is None:
            return 60 + 1.55 * a[2]
        if k is None:
            k = 0.5 if SCRATCH[o[3]][2] == SCRATCH[a[3]][2] == "bfloat16" else 1.0
        return 60 + 1.04 * max(64, k * a[2])

    def add(q, fn, rd, wr, ns, kind="c", extra=None):
        ops.append({"q": q, "fn": fn, "rd": rd, "wr": wr, "ns": ns, "kind": kind, "extra": extra, "at": phase[0]})

    def tt(o, a, b, op):
        k = 1.0 if (str(a[3]).startswith("pb") or b[3].startswith("pb")) else 2.0
        add("v", lambda e: e.tensor_tensor(o[0], a[0], b[0], op), fp(a, b), fp(o), span(o, a, k))

    def ts(o, a, s1, op0, s2=None, op1=None):
        if op1 is None:
            add("v", lambda e: e.tensor_scalar(o[0], a[0], val(s1), None, op0), fp(a, s1), fp(o), span(o, a))
        else:
            add("v", lambda e: e.tensor_scalar(o[0], a[0], val(s1), val(s2), op0, op1), fp(a, s1, s2), fp(o), span(o, a))

    def cp(o, a):
        add("v", lambda e: e.tensor_copy(o[0], a[0]), fp(a), fp(o), span(o, a))

    def ms(o, c):
        add("v", lambda e: e.memset(o[0], c), [], fp(o), span(o, o))

    def act(o, a, f=F.Identity, bias=0.0, scale=1.0, acc=None):
        if acc is None:
            add("s", lambda e: e.activation(o[0], a[0], f, bias=val(bias), scale=val(scale)), fp(a, bias, scale), fp(o), span(o, a, 1.0))
        else:
            add("s", lambda e: e.activation(o[0], a[0], f, bias=val(bias), scale=val(scale), accum_out=acc[0]),
                fp(a, bias, scale), fp(o, acc), span(o, a, 1.0))

    def mm(o, l, r, st=True, sp=True):
        add("t", lambda e: e.matmul(o[0], l[0], r[0], st, sp), fp(l, r), fp(o), 0.55 * max(64, r[2]))

    def iota(o, pat, base, cm, small=False):
        if small:
            add("g", lambda e: e.iota(o[0], pat, base, cm, allow_small_or_imprecise_dtypes=True), [], fp(o), 130 + 2.1 * o[2])
        else:
            add("g", lambda e: e.iota(o[0], pat, base, cm), [], fp(o), 130 + 2.1 * o[2])

    nd = [0]

    def dma(q, o, a, ns=2500):
        s = "d%d" % nd[0]
        nd[0] += 1
        add(q, lambda e: e.dma_start(o[0], a[0]), fp(a), fp(o), ns, "d", s)

    def X(ap):
        return (ap, [])

    mine = [q for q, c in enumerate(T.cores) if topo.chip(c) == topo.chip(core)]
    other = [q for q, c in enumerate(T.cores) if topo.chip(c) != topo.chip(core)]
    partner = other[mine.index(me)]
    mates = [q for q in mine if q != me]
    far = topo.mask(core, T.cores[partner])
    near = topo.mask(core, T.cores[mates[0]])
    rest = near & ~far

    def cnt(m):
        return bin(m).count("1")

    def dst(q):
        a = topo.addr(T.cores[q])
        return DstId(rid=a[0], pnc=a[1])

    nx = [0]

    def send(buf, base, w, src=None):
        i = nx[0]
        nx[0] += 1
        xa, xb, xl, xf = ("xa%d" % i, "xb%d" % i, "xl%d" % i, "xf%d" % i)

        def slot(q):
            return R(buf, base + w * q, base + w * (q + 1))
        own = slot(me)
        src = own if src is None else src
        par = slot(partner)

        def f1(e):
            return e.remote_dma_fused([
                RemoteDMATransfer(dst_ids=[dst(partner)], dma_engine_mask=far, remote_sem=T.sem[xa], srcs=[src[0]], dsts=[own[0]]),
                RemoteDMATransfer(dst_ids=[dst(q) for q in mates], dma_engine_mask=rest, remote_sem=T.sem[xb], srcs=[src[0]],
                                  dsts=[own[0] for q in mates])], local_sem=T.sem[xl])

        def f2(e):
            return e.remote_dma_fused([
                RemoteDMATransfer(dst_ids=[dst(q) for q in mates], dma_engine_mask=near, remote_sem=T.sem[xb], srcs=[par[0]],
                                  dsts=[par[0] for q in mates])], local_sem=T.sem[xf])
        add("g", f1, fp(src), [], 3000, "r", (xl, cnt(far) + cnt(rest)))
        add(None, None, [], fp(par), len(ops) - 1, "a", (xa, cnt(far)))
        add("g", f2, fp(par), [], 3000, "r", (xf, cnt(near)))
        add(None, None, [], fp(*[slot(q) for q in range(len(T.cores)) if q not in (me, partner)]), len(ops) - 1, "a",
            (xb, len(mates) * (cnt(rest) + cnt(near))))

    def sel(n, base, p):
        return R(n, base + 15 - p, base + 143 - p)

    def every16(src, lo, hi, p):
        return (T[src][:, lo + p:hi:16], [(src, lo, hi, 1, 0)], (hi - lo) // 16, src)

    def to_list(o, n, base, src, lo, hi, first=True):
        for p in range(16):
            mm(o, sel(n, base, p), every16(src, lo, hi, p), first and p == 0, p == 15)

    def col(i):
        return R("COL", i, i + 1)

    def eye(n):
        return R(n, 0, 128)

    own0 = 1024 + 128 * me
    dma("y", R("H0", own0, own0 + 128), X(T.h0[:, 0:128]))
    dma("s", R("NB", 0, 256), X(T.nb[:]))
    dma("y", R("H0", 0, 1024), X(T.h0[:]))
    dma("y", R("HO0", 0, 1024), X(T.h0[:]))
    iota(R("KC", 0, 1), [[0, 1]], 0, 1)
    iota(R("J", 0, 144), [[1, 144]], 0, 0, True)
    iota(U("VI", 0, 4), [[0, 4], [16, 64]], 0, 0)
    at = len(ops)
    iota(R("JG", 0, 128), [[16, 8], [0, 16]], 0, 0, True)
    iota(R("JR", 0, 128), [[0, 8], [1, 16]], 0, 0, True)
    iota(U("PRI", 0, 4), [[1, 4], [0, 64]], 0, 0)
    early = ops[at:]
    del ops[at:]
    send("H0", 1024, 128)
    ops[at + 2:at + 2] = early
    ops[-1]["ns"] = len(ops) - 2
    iota(U("CB", 0, 8), [[1, 8], [0, 64]], 1, 0, True)
    iota(U("CC", 0, 4), [[2, 4], [0, 64]], -7, 0, True)
    iota(U("CC", 4, 8), [[2, 4], [0, 64]], -1, 0, True)
    ms(R("H0", 2048, 4096), -1.0)
    ts(R("KC", 1, 2), R("KC", 0, 1), 15, A.bitwise_and)
    cp(R("COL", 0, 2), R("KC", 0, 2))
    tt(col(2), col(0), col(1), A.subtract)
    ts(col(3), col(2), 15.0, A.add)
    ts(col(4), col(1), 4.0, A.is_lt)
    ts(R("EQ", 0, 16), R("J", 0, 16), col(1), A.is_equal)
    ts(R("D", 0, 144), R("J", 0, 144), col(3), A.is_equal)
    ts(col(7), col(4), 10.0, A.mult)
    tt(col(5), col(7), R("EQ", 5, 6), A.add)
    bias = []
    for r in range(RO):
        c = col(7)
        for l in range(4):
            if ASR[r][l] == "s":
                ts(col(16 + r), R("EQ", l, l + 1), -8.0, A.mult, c, A.add)
                c = col(16 + r)
        bias.append(c)
    act(R("DN", 0, 144), R("D", 0, 144), scale=-1.0)
    ts(U("T4", 0, 4), R("NB", 0, 256), 3, A.arith_shift_right, 896, A.bitwise_and)
    ts(U("U4", 0, 4), R("NB", 0, 256), 1023, A.bitwise_and)
    ts(U("V4", 0, 4), U("VI", 0, 4), col(1), A.add)
    ts(P(0, 0, 4), U("T4", 0, 4), 1024.0, A.add)
    ts(U("W4", 0, 4), U("U4", 0, 4), 128.0, A.is_lt)
    ts(P(1, 0, 4), U("V4", 0, 4), 128.0, A.is_lt, float(own0), A.mult)
    tt(P(0, 4, 8), P(0, 0, 4), U("W4", 0, 4), A.mult)
    tt(P(1, 4, 8), P(1, 0, 4), U("V4", 0, 4), A.add)
    tt(U("NM", 0, 4), P(0, 4, 8), U("U4", 0, 4), A.add)
    tt(U("T4", 0, 4), P(1, 4, 8), U("NM", 0, 4), A.is_equal)
    ts(P(0, 0, 4), U("T4", 0, 4), 2048.0, A.mult)
    tt(U("N8", 0, 4), P(0, 0, 4), U("NM", 0, 4), A.add)
    cp(R("OA", 0, 256), U("N8", 0, 4))
    act(U("ME", 0, 4), P(1, 4, 8))
    act(U("EMP", 0, 4), P(1, 4, 8), bias=2048.0 + 2 ** 17 + 2 ** 16)
    ts(R("PA", 0, 128), R("JR", 0, 128), 4.0, A.is_equal)
    ts(col(6), R("EQ", 5, 6), -64.0, A.mult)
    ts(col(8), col(4), 127.0, A.mult, col(6), A.add)
    ts(R("PA", 0, 128), R("PA", 0, 128), col(8), A.mult, col(4), A.add)
    ts(R("WOULD", 0, 128), R("JG", 0, 128), col(2), A.is_equal)
    tt(R("BL", 0, 128), R("WOULD", 0, 128), R("PA", 0, 128), A.mult)
    ts(eye("ID"), R("J", 0, 128), col(0), A.is_equal)
    ms(R("ONE", 0, 128), 1.0)
    ms(R("DB", 0, 128), 0.0)
    ms(U("NL", 0), 0.0)
    ts(col(9), col(1), -31.5, A.add)
    ts(col(10), col(1), -15.5, A.add)
    ts(col(11), R("EQ", 4, 5), 65536.0, A.mult)
    ts(col(12), col(4), -2.0 * BIG, A.mult, col(11), A.add)
    ts(R("WR", 8, 12), R("EQ", 8, 12), 16384.0, A.mult)
    ts(R("C8", 0, 4), R("J", 0, 4), 256.0, A.mult, 128.0, A.add)
    tt(R("WR", 4, 8), R("EQ", 4, 8), R("EQ", 0, 4), A.add)
    ts(U("PRI", 0, 4), U("PRI", 0, 4), float(4096 - 2 ** 22), A.mult, float(3 * 2 ** 22 + 4096 + 32 * 65536), A.add)
    tt(R("WR", 0, 4), R("WR", 4, 8), R("WR", 8, 12), A.add)
    ms(R("TAB0", 2048, 4096), 1.0)
    ms(R("WB", 512, 528), 0.0)
    ms(R("PL0", 0, 128), 0.0)
    ms(R("PL1", 0, 128), 0.0)
    ms(R("PL0", 3072, 4096), 0.0)
    for p in range(16):
        act(R("WP", 144 * p, 144 * p + 144), R("D", 0, 144), scale=R("EQ", p, p + 1))
    act(R("DH", 0, 144), R("D", 0, 144), scale=-0.5)
    act(R("DT", 0, 144), R("D", 0, 144), scale=col(12))
    act(R("DA", 0, 144), R("D", 0, 144), scale=col(4))
    act(R("DS", 0, 144), R("D", 0, 144), scale=4096.0)
    for l in range(4):
        act(R("DR", 144 * l, 144 * l + 144), R("D", 0, 144), scale=R("WR", l, l + 1))
    for n, s in (("IN", -1.0), ("IH", 0.5), ("KP", BIG), ("KN", -BIG), ("HP", BIG / 2), ("HM", -BIG / 2), ("RP", RK), ("RN", -RK),
                 ("I4", 4096.0), ("IC", RK + 4096.0)):
        act(eye(n), eye("ID"), scale=s)
    add("y", None, fp(R("H0", 1024, 2048)), [], 0, "w")
    dma("y", R("PL0", 4096, 8192), X(T.w0[:]), 6000)
    dma("y", R("TAB1", 2048, 4096), R("TAB0", 2048, 4096))
    dma("y", R("TAB2", 2048, 4096), R("TAB0", 2048, 4096))
    dma("y", R("H1", 2048, 4096), R("H0", 2048, 4096))
    dma("y", R("H2", 2048, 4096), R("H0", 2048, 4096))
    dma("y", R("PL1", 3072, 4096), R("PL0", 3072, 4096))
    ID, IN, KP, KN = eye("ID"), eye("IN"), eye("KP"), eye("KN")
    halves = ((128, 576), (576, 1024))
    off = [0]
    for d in range(1, 8):
        off.append(off[-1] + 8 - d)

    def sums(c, src, lo):
        for p in range(16):
            mm(P(3, c), sel("DS", 0, p), every16(src, lo, lo + 1024, p), p == 0, False)
        mm(P(3, c), KP, U("P2", c), False, False)
        mm(P(3, c), KP, U("P1", c), False, True)

    for r in range(RO):
        H, HX, HO, HN, TAB = "H%d" % r, "H%d" % (r + 1), "HO%d" % r, "HO%d" % (r + 1), "TAB%d" % r
        PL, PX = "PL%d" % (r % 2), "PL%d" % ((r + 1) % 2)
        HW = R(H, 0, 4096)
        last = r == RO - 1
        ASL = ASR[r]
        phase[0] = 4 * r + 1
        for l in range(4):
            tt(R("CMP", 1024 * l, 1024 * l + 128), IND(HW, R("OA", 64 * l, 64 * l + 8)), R(HO, 0, 128), A.is_lt)
        for l in range(4):
            mm(P(4, 0, 2), sel("DN", 0, l), R("CMP", 1024 * l, 1024 * l + 128), l == 0, l == 3)
        act(R("FB", 0, 128), P(4, 0, 2), F.Relu, bias=col(5))
        mm(P(4, 2, 4), R("BL", 0, 128), R("FB", 0, 128))
        tt(R("WOULD", 0, 128), P(4, 2, 4), R("DB", 0, 128), A.is_le)
        add("v", lambda e: e.tensor_tensor_scan(T.CUM[:, :], T.ONE[:, :], T.WOULD[:, :], -32.0, A.mult, A.add),
            fp(R("ONE", 0, 128), R("WOULD", 0, 128)), fp(R("CUM", 0, 128)), 200)
        tt(R(TAB, own0, own0 + 128), R("CUM", 0, 128), P(4, 2, 4), A.max)
        send(TAB, 1024, 128)
        cp(U("P1", 0, 4), U("N8", 0, 4))
        tt(U("P2", 0, 4), U("N8", 0, 4), U("P1", 0, 4), A.subtract)
        for h in range(2):
            for p in range(8 * h, 8 * h + 8):
                for f in range(8):
                    mm(P(6 + h, p % 8), sel("WP", 144 * p, f), U("P%d" % (1 + f // 4), f % 4), f == 0, f == 7)
            for p in range(8 * h, 8 * h + 8):
                act(R("NAT", p, 1024, 16), P(6 + h, p % 8))
        phase[0] = 4 * r + 2
        seq = [l for l in range(4) if ASL[l] == "v"]
        seq = seq[:-1] + [l for l in range(4) if ASL[l] == "s"] + seq[-1:]
        for h, (a, b) in enumerate(halves):
            for n, l in enumerate(seq):
                c, src = R("CMP", 1024 * l + a, 1024 * l + b), IND(HW, R("OA", 64 * l + a // 16, 64 * l + b // 16))
                if ASL[l] == "v":
                    tt(c, src, R(HO, a, b), A.is_lt)
                else:
                    hn = R("HN", 896 * (l % 2) + a - 128, 896 * (l % 2) + b - 128)
                    act(hn, src)
                    mm(P(2 + l % 2, 0, 7), ID, R(HO, a, b), True, False)
                    mm(P(2 + l % 2, 0, 7), IN, hn, False, True)
                    act(c, P(2 + l % 2, 0, 7), F.Sign, bias=-0.5)
                mm(P(h, 0, 7), sel("DN" if ASL[l] == "v" else "DH", 0, l), c, n == 0, n == 3)
        for h in range(2):
            act(R("JUNK", 0, 128), R("CUM", 0, 128), F.Sign, bias=col(9 + h), scale=-1.0, acc=R("ACC", 4 * h, 4 * h + 1))
        act(R(TAB, 0, 128), R(TAB, own0, own0 + 128))
        for h in range(2):
            ts(R("OC", h, 8, 2), R("C8", 0, 4), R("ACC", 4 * h, 4 * h + 1), A.add, 0.5, A.mult)
        if not last:
            ts(R("PA", 0, 128), R(TAB, own0, own0 + 128), -1.0, A.add, 1000.0, A.mult)
            tt(R("DB", 0, 128), R("PA", 0, 128), R("DB", 0, 128), A.min)
        ts(R(TAB, 128, 576), P(0, 0, 7), bias[r], A.add, 0.0, A.max)
        act(R(TAB, 576, 1024), P(1, 0, 7), F.Relu, bias=bias[r])
        e3 = 1024 + 256 * me
        if r == 0:
            for l in range(4):
                act(R("WB", 128 * l, 128 * l + 128), R(PL, 4096 + 1024 * l, 4224 + 1024 * l))
        act(R(PL, e3 + 128, e3 + 256), IND(R("WB", 0, 528), R("OC", 0, 8)))
        to_list(P(4, 4), "DT", 0, TAB, 0, 1024)
        tt(U("SP", 0, 4), U("N8", 0, 4), U("PRI", 0, 4), A.add)
        ts(U("NL", 1), P(4, 4), -BIG, A.is_gt, BIG, A.mult)
        tt(U("NL", 0), U("NL", 0), U("NL", 1), A.max)
        for l in range(4):
            sums(l, PL, 4096 + 1024 * l)
        act(U("Z", 0, 4), P(3, 0, 4))
        TW = R(TAB, 0, 4096)

        def gone(l, k, a, b):
            o, i = R("G", 1024 * l + a, 1024 * l + b), IND(TW, R("OA", 64 * l + a // 16, 64 * l + b // 16))
            if GS[k][l] == "v":
                cp(o, i)
            else:
                act(o, i)
        for l in range(4):
            gone(l, 0, 0, 128)
        mm(P(5, 0, 2), ID, R("NAT", 0, 128), True, False)
        for l in range(4):
            mm(P(5, 0, 2), sel("DA", 0, 8 + l), R("G", 1024 * l, 1024 * l + 128), False, l == 3)
        act(R(PL, e3, e3 + 128), P(5, 0, 2))
        send(PL, 1024, 256)
        phase[0] = 4 * r + 3
        for h, (a, b) in enumerate(halves):
            mm(P(h, 0, 7), ID, R("NAT", a, b), True, False)
        for l in (0, 2, 1, 3):
            gone(l, 1, 128, 576)
            gone(l, 2, 576, 1024)
            mm(P(4, l), IN, U("NL", 0), True, False)
            to_list(P(4, l), "DT", 0, "G", 1024 * l, 1024 * l + 1024, False)
            for h, (a, b) in enumerate(halves):
                mm(P(h, 0, 7), sel("DA", 0, 8 + l), R("G", 1024 * l + a, 1024 * l + b), False, l == 3)
        for h, (a, b) in enumerate(halves):
            act(R(PL, a, b), P(h, 0, 7))
        tt(U("X", 0, 4), P(4, 0, 4), U("SP", 0, 4), A.add)
        tt(U("SM", 0, 2), U("X", 0, 2), U("X", 2, 4), A.max)
        tt(U("SM", 3), U("SM", 0), U("SM", 1), A.max)
        ts(U("SI", 0), U("SM", 3), 0.0, A.max)
        ts(U("SI", 1), U("SI", 0), 2, A.arith_shift_right, 7168, A.bitwise_and)
        ts(U("SI", 2), U("SI", 0), 2047, A.bitwise_and)
        tt(U("SM", 4), U("SI", 1), U("V4", 0), A.add)
        cp(R("OS", 0, 64), U("SM", 4))
        act(R("WS", 0, 1024), IND(R(PL, 3072, 8192), R("OS", 0, 64)))
        ts(U("SI", 3), U("SI", 2), -1024.0, A.add, 0.0, A.max)
        ts(U("SI", 4), U("SI", 3), 896, A.bitwise_and)
        cp(R("OD", 0, 64), U("SI", 2))
        ts(U("SI", 5), U("SI", 0), 16, A.arith_shift_right, 63, A.bitwise_and)
        tt(U("SM", 5), U("SI", 2), U("SI", 4), A.add)
        cp(R("OI", 0, 64), U("SM", 5))
        act(R("IG", 0, 1024), IND(R(PL, 0, 3072), R("OI", 0, 64)))
        ts(U("SM", 6), U("SI", 4), 2.0, A.mult, 127.0 - 3072.0, A.add)
        ts(U("SM", 7), U("SI", 2), 1024.0, A.is_ge)
        tt(U("SM", 8), U("SI", 5), U("SI", 2), A.subtract)
        tt(U("SM", 10), U("SM", 6), U("SM", 8), A.add)
        tt(U("SM", 11), U("SM", 10), U("SM", 7), A.mult)
        ts(U("SM", 12), U("SI", 2), 3072.0, A.add)
        ts(U("SM", 13), U("SM", 7), -992.0, A.mult, 1024.0, A.add)
        tt(U("PT", 0), U("SM", 11), U("SM", 12), A.add)
        ts(U("SM", 14), U("SM", 7), -1984.0, A.mult, 2048.0, A.add)
        tt(U("PT", 1), U("PT", 0), U("SM", 13), A.add)
        cp(R("OW", 0, 128), U("PT", 0, 2))
        tt(U("PT", 2), U("PT", 0), U("SM", 14), A.add)
        tt(U("PT", 3), U("PT", 1), U("SM", 14), A.add)
        cp(R("OW", 128, 256), U("PT", 2, 4))
        ts(U("SM", 9), U("SI", 4), float(128 * me), A.not_equal, 1024.0, A.mult)
        tt(U("SB", 1), U("SM", 9), U("SM", 7), A.mult)
        ts(U("SB", 2), U("SM", 3), 0.0, A.is_ge, 2.0 ** -8, A.add)
        act(U("SB", 3), U("SM", 3), F.Relu, scale=-1.0)
        act(U("F2", 0, 4), U("X", 0, 4), F.Relu, bias=1.0)
        tt(R("NE", 0, 1024), IND(R(H, 0, 2048), R("OD", 0, 64)), R("WS", 0, 1024), A.subtract)
        for l in range(4):
            mm(P(4, l), KP, U("SB", 2), True, False)
            mm(P(4, l), eye("I4"), U("CB", l), False, True)
            mm(P(5, 4 + l), ID, U("SB", 1))
        mm(P(7, 0, 4), ID, U("P1", 0, 4), True, False)
        mm(P(7, 0, 4), ID, U("P2", 0, 4), False, True)
        tt(P(4, 4, 8), P(4, 0, 4), U("N8", 0, 4), A.add)
        tt(U("FILL", 0, 4), P(4, 4, 8), U("EMP", 0, 4), A.min)
        for h in range(2):
            mm(P(h, 0, 8), ID, R("WS", 512 * h, 512 * h + 512), True, False)
            mm(P(h, 0, 8), IN, R(HO, 512 * h, 512 * h + 512), False, True)
            ts(R("Q", 512 * h, 512 * h + 512), P(h, 0, 8), 0.0, A.max, 255.5, A.add)
            mm(P(h, 0, 8), ID, R(HO, 512 * h, 512 * h + 512), True, False)
            mm(P(h, 0, 8), eye("IH"), R("Q", 512 * h, 512 * h + 512), False, True)
            act(R(HN, 512 * h, 512 * h + 512), P(h, 0, 8), bias=-128.0)
        if last:
            dma("y", X(T.yh[:]), R(HN, 0, 1024))
        else:
            send(HX, 1024, 128, R(HN, 0, 128))
            dma("y", R(HX, 0, 1024), R(HN, 0, 1024))
            dma("y", R(HX, own0, own0 + 128), R(HN, 0, 128))
        phase[0] = 4 * r + 4
        for l in range(4):
            to_list(P(5, l), "DR", 144 * l, "IG", 0, 1024)
        cp(U("RI", 0, 4), P(5, 0, 4))
        ts(U("NM", 0, 4), U("RI", 0, 4), 4095, A.bitwise_and)
        tt(U("V3", 0, 4), P(5, 4, 8), U("NM", 0, 4), A.is_le)
        act(U("F2", 4, 8), P(5, 0, 4), F.Relu, scale=-1.0, bias=16384.0)
        tt(P(7, 4, 8), U("NM", 0, 4), U("V3", 0, 4), A.mult)
        cp(U("N8", 4, 8), P(7, 4, 8))
        tt(U("FL", 4, 8), P(7, 4, 8), U("ME", 0, 4), A.is_equal)
        cp(U("P1", 4, 8), P(7, 4, 8))
        tt(U("P2", 4, 8), P(7, 4, 8), U("P1", 4, 8), A.subtract)
        mm(P(6, 0, 8), eye("HP"), U("CC", 0, 8), True, False)
        for k in range(8):
            mm(P(6, k), KN, U("SB", 3), False, False)
        mm(P(6, 0, 8), KN, U("F2", 0, 8), False, False)
        mm(P(6, 4, 8), KP, U("V3", 0, 4), False, False)
        act(U("KF", 0, 8), P(7, 0, 8), F.Relu, bias=-2047.0)
        mm(P(6, 4, 8), KN, U("FL", 4, 8), False, False)
        mm(P(6, 0, 8), KN, U("KF", 0, 8), False, False)
        mm(P(6, 0, 8), KN, U("P1", 0, 8), False, False)
        mm(P(6, 0, 8), KN, U("P2", 0, 8), False, False)
        for d in range(1, 8):
            tt(U("O1", off[d - 1], off[d]), P(7, 0, 8 - d), U("N8", d, 8), A.subtract)
        for a, b in SG:
            act(U("O4", off[a], off[b]), U("O1", off[a], off[b]), F.Sign, bias=-0.5)
            act(U("O2", off[a], off[b]), U("O1", off[a], off[b]), F.Sign, bias=0.5)
        for d in range(1, 8):
            mm(P(6, d, 8), eye("HP"), U("O4", off[d - 1], off[d]), False, False)
            mm(P(6, 0, 8 - d), eye("HM"), U("O2", off[d - 1], off[d]), False, False)
        mm(P(5, 0, 8), eye("IC"), U("CB", 0, 8), True, False)
        mm(P(5, 0, 8), ID, U("P1", 0, 8), False, False)
        mm(P(5, 0, 8), ID, U("P2", 0, 8), False, False)
        PWIN = R(PL, 1024, 8192)
        bank = 0
        for l in range(4):
            a = 8192 + 1024 * l
            wd, src = R("WD", 1024 * l, 1024 * l + 1024), IND(PWIN, R("OW", 64 * l, 64 * l + 64))
            if MODE[l] == "f":
                tt(wd, src, R("NE", 0, 1024), A.subtract)
                ts(R(PL, a, a + 1024), wd, 0.0, A.max, 255.0, A.min)
            else:
                act(wd, src)
                for h in range(2):
                    mm(P(bank, 0, 8), ID, R("WD", 1024 * l + 512 * h, 1024 * l + 512 * h + 512), True, False)
                    mm(P(bank, 0, 8), IN, R("NE", 512 * h, 512 * h + 512), False, True)
                    ts(R(PL, a + 512 * h, a + 512 * h + 512), P(bank, 0, 8), 0.0, A.max, 255.0, A.min)
                    bank = (bank + 1) % 3
            sums(4 + l, PL, a)
        cp(U("Z", 4, 8), P(3, 4, 8))
        for d in range(1, 8):
            tt(U("O3", off[d - 1], off[d]), P(3, 0, 8 - d), U("Z", d, 8), A.is_ge)
            mm(P(6, d, 8), KN, U("O3", off[d - 1], off[d]), False, False)
            mm(P(6, 0, 8 - d), KP, U("O3", off[d - 1], off[d]), False, d == 7)
        tt(U("KS", 0, 8), P(6, 0, 8), U("Z", 0, 8), A.add)
        tt(P(4, 0, 8), P(6, 0, 8), U("Z", 0, 8), A.add)
        act(U("KF", 0, 8), U("KS", 0, 8), F.Relu, scale=-1.0)
        mm(P(5, 0, 8), IN, U("KF", 0, 8), False, False)
        for d in range(1, 8):
            tt(U("O1", off[d - 1], off[d]), P(4, 0, 8 - d), U("KS", d, 8), A.is_ge)
            mm(P(5, d, 8), eye("RN"), U("O1", off[d - 1], off[d]), False, False)
            mm(P(5, 0, 8 - d), eye("RP"), U("O1", off[d - 1], off[d]), False, d == 7)
        for k in range(4):
            act(P(k, 0, 4), P(5, 0, 4), F.Abs, bias=RK * (k - 8))
            act(U("AS", 4 * k, 4 * k + 4), P(5, 4, 8), F.Abs, bias=RK * (k - 8))
            tt(P(6, 2 * k, 2 * k + 2), P(k, 0, 2), U("AS", 4 * k, 4 * k + 2), A.min)
            tt(U("L1", 2 * k, 2 * k + 2), P(k, 2, 4), U("AS", 4 * k + 2, 4 * k + 4), A.min)
        tt(P(7, 0, 4), P(6, 0, 8, 2), U("L1", 0, 8, 2), A.min)
        tt(U("L2", 0, 4), P(6, 1, 8, 2), U("L1", 1, 8, 2), A.min)
        tt(P(7, 4, 8), P(7, 0, 4), U("FILL", 0, 4), A.min)
        tt(U("S16", 0, 4), P(7, 4, 8), U("L2", 0, 4), A.min)
        if not last:
            ts(U("N8", 0, 4), U("S16", 0, 4), 4095, A.bitwise_and)
            cp(R("OA", 0, 256), U("N8", 0, 4))
        ts(U("T4", 0, 4), U("S16", 0, 4), 2, A.arith_shift_right, 15360, A.bitwise_and)
        tt(U("PT", 0, 4), U("T4", 0, 4), U("V4", 0, 4), A.add)
        cp(R("OP", 0, 256), U("PT", 0, 4))
        if last:
            ts(U("N8", 0, 4), U("S16", 0, 4), 2047, A.bitwise_and)
        else:
            for l in range(4):
                act(R("WB", 128 * l, 128 * l + 128), IND(R(PL, 3072, 12288), R("OP", 64 * l, 64 * l + 8)))
        for l in range(4):
            for a in (1024 * l, 1024 * l + 512):
                o, i = R(PX, 4096 + a, 4608 + a), IND(R(PL, 3072, 12288), R("OP", a // 16, a // 16 + 32))
                if last and l % 2:
                    cp(o, i)
                else:
                    act(o, i)
        if last:
            for a in (0, 1024, 512, 1536, 2048, 3072, 2560, 3584):
                dma("y", X(T.yw[:, a:a + 512]), R(PX, 4096 + a, 4608 + a))
    ts(U("T4", 0, 4), U("N8", 0, 4), -1024.0, A.add, 0.0, A.max)
    ts(P(0, 0, 4), U("N8", 0, 4), 1024.0, A.is_ge, float(-1024 - 1024 * me), A.mult)
    ts(U("U4", 0, 4), U("T4", 0, 4), 896, A.bitwise_and)
    tt(U("X", 0, 4), P(0, 0, 4), U("N8", 0, 4), A.add)
    ts(P(0, 4, 8), U("U4", 0, 4), 7.0, A.mult, float(1024 * me), A.add)
    tt(R("YN", 0, 256), P(0, 4, 8), U("X", 0, 4), A.add)
    dma("s", X(T.yn[:]), R("YN", 0, 256))
    return ops


def links(ops):
    hist = {}
    lastq = {}
    deps, soft = [], []
    for i, o in enumerate(ops):
        need, keepo = set(), set()
        for w, fps in ((False, o["rd"]), (True, o["wr"])):
            for (n, lo, hi, m, c) in fps:
                ps = n.startswith("pb")
                keep = []
                if ps and hist.get(n) and hist[n][0][0] != i and ops[hist[n][0][0]]["q"] == o["q"]:
                    keepo.add(hist[n][0][0])
                for x in hist.get(n, []):
                    j, jw, jlo, jhi, jm, jc = x
                    hit = jlo < hi and lo < jhi and not (m == jm and c != jc)
                    same = ops[j]["q"] == o["q"]
                    if j != i:
                        if ps and same and o["q"] == "t":
                            keepo.add(j)
                        elif (hit and (w or jw)) or (ps and not same):
                            need.add(j)
                    if ps:
                        if same and o["q"] != "t":
                            keep.append(x)
                    elif not (w and m == 1 and lo <= jlo and jhi <= hi):
                        keep.append(x)
                keep.append((i, w, lo, hi, m, c))
                hist[n] = keep
        if o["q"] in ("g", "y"):
            if o["q"] in lastq:
                keepo.add(lastq[o["q"]])
            lastq[o["q"]] = i
        if o["kind"] == "a":
            need, keepo = set(), {o["ns"]}
        deps.append(need)
        soft.append(keepo)
    return deps, soft


def tag(o):
    return (o["q"] + o["wr"][0][0], o["at"]) if o["wr"] and o["q"] else None


def arrange(ops, deps, soft, bonus):
    n = len(ops)
    hold = [0.0 if o["kind"] == "a" else (300.0 if o["kind"] == "r" else (60.0 if o["kind"] == "d" else o["ns"])) for o in ops]
    done = [0.0 if o["kind"] == "a" else o["ns"] for o in ops]
    succ = [[] for _ in ops]
    left = [0] * n
    for i in range(n):
        for j in deps[i] | soft[i]:
            succ[j].append((i, done[j] + 60.0 if (j in deps[i] or ops[i]["kind"] == "a") else hold[j]))
            left[i] += 1
    way = [0.0] * n
    for j in range(n - 1, -1, -1):
        way[j] = max([done[j]] + [lag + way[i] for i, lag in succ[j]]) + bonus.get(tag(ops[j]), 0)
    can = [0.0] * n
    ready = {}
    free = {}
    for i in range(n):
        if not left[i]:
            ready.setdefault(ops[i]["q"], []).append(i)
    order = []
    while len(order) < n:
        best = None
        for q, l in ready.items():
            if l:
                t = max(free.get(q, 0.0), min(can[i] for i in l))
                if best is None or t < best[0]:
                    best = (t, q)
        t, q = best
        i = max((i for i in ready[q] if can[i] <= t + 40.0), key=lambda i: (way[i], -i))
        t = max(t, can[i])
        ready[q].remove(i)
        order.append(i)
        free[q] = t + hold[i]
        for k, lag in succ[i]:
            can[k] = max(can[k], t + lag)
            left[k] -= 1
            if not left[k]:
                ready.setdefault(ops[k]["q"], []).append(k)
    return order


def length(ops, deps, seq, gath, f, fg, hop):
    end, free = {}, {}
    for i in seq:
        o = ops[i]
        k = o["kind"]
        if k == "a":
            end[i] = end[o["ns"]]
            continue
        t = free.get(o["q"], 0.0)
        for j in deps[i]:
            if end[j] + 60.0 > t:
                t = end[j] + 60.0
        if k == "c":
            d = o["ns"] * f if o["q"] == "t" else 60.0 + (o["ns"] - 60.0) * (fg if gath[i] else f)
            free[o["q"]] = end[i] = t + d
        elif k == "r":
            free["g"], end[i] = t + 300.0, t + hop
        elif k == "d":
            free[o["q"]], end[i] = t + 50.0, t + o["ns"]
        else:
            free[o["q"]] = end[i] = t
    return max(end.values())


def plan(ops, deps, soft):
    if "bonus" not in PLAN:
        gath = [any(SCRATCH[x[0]][2] == "uint16" for x in o["rd"]) for o in ops]
        keys = sorted({tag(o) for o in ops if o["wr"] and o["q"] in ("v", "s", "t")})

        def cost(b):
            seq = arrange(ops, deps, soft, b)
            return (length(ops, deps, seq, gath, 0.8, 0.8, 2300.0) / 142 + length(ops, deps, seq, gath, 1.15, 1.55, 3600.0) / 212
                    + length(ops, deps, seq, gath, 1.0, 0.75, 3000.0) / 160)
        b = {k: BONUS.get(k[0], 0) for k in keys}
        best = cost(b)
        x = 12345
        for _ in range(TRIES):
            c = dict(b)
            for _k in range(1 + (x >> 8) % 3):
                x = (x * 1103515245 + 12345) % 2147483648
                k = keys[(x >> 8) % len(keys)]
                x = (x * 1103515245 + 12345) % 2147483648
                c[k] += (-1500, -600, -250, 250, 600, 1500, 3000)[(x >> 8) % 7]
            v = cost(c)
            if v < best:
                best, b = v, c
        PLAN["bonus"] = b
    return PLAN["bonus"]


def emit(g, T, ops):
    eng = {"v": g.vector, "s": g.scalar, "t": g.tensor, "g": g, "y": g.sync}
    deps, soft = links(ops)
    seq = arrange(ops, deps, soft, plan(ops, deps, soft))
    order, cnt, place = {}, {}, {}
    for n, i in enumerate(seq):
        place[i] = n
        if ops[i]["kind"] == "c":
            cnt[ops[i]["q"]] = cnt.get(ops[i]["q"], 0) + 1
            order[i] = cnt[ops[i]["q"]]
    known = {q: {} for q in eng}
    after, waits, used = {}, {}, set()
    for i in seq:
        o = ops[i]
        if o["kind"] == "a":
            continue
        kn = known[o["q"]]
        want = {}
        for j in deps[i]:
            p = ops[j]
            if p["kind"] == "c":
                key, v = p["q"], order[j]
            elif p["kind"] == "w":
                continue
            else:
                key, v = ("x", j), 1
            if want.get(key, (0, 0))[0] < v:
                want[key] = (v, j)
        ws = []
        for key, (v, j) in sorted(want.items(), key=lambda t: -place[t[1][1]]):
            if kn.get(key, 0) >= v:
                continue
            ws.append(j)
            used.add(j)
            kn[key] = v
            for k2, v2 in after.get(j, {}).items():
                if kn.get(k2, 0) < v2:
                    kn[k2] = v2
        waits[i] = ws
        after[i] = dict(kn)
    tick, token = {}, {}
    for i in seq:
        o = ops[i]
        if o["kind"] == "c" and i in used:
            tick[o["q"]] = tick.get(o["q"], 0) + 1
            token[i] = ("q" + o["q"], tick[o["q"]])
        elif o["kind"] == "d":
            token[i] = (o["extra"], 16)
        elif o["kind"] in ("a", "r"):
            token[i] = o["extra"]
    sent = []
    for i in seq:
        o = ops[i]
        if o["kind"] == "a":
            continue
        e = eng[o["q"]]
        for j in waits[i]:
            e.wait_ge(T.sem[token[j][0]], token[j][1])
        if o["kind"] == "r":
            while len(sent) > 2:
                t = sent.pop(0)
                e.wait_ge(T.sem[t[0]], t[1])
            sent.append(token[i])
        if o["fn"] is None:
            continue
        ins = o["fn"](e)
        if o["kind"] == "d":
            ins.then_inc(T.sem[token[i][0]], 16)
        elif o["kind"] == "c" and i in used:
            ins.then_inc(T.sem[token[i][0]], 1)
    for i in seq:
        if ops[i]["kind"] in ("d", "a", "r"):
            g.wait_ge(T.sem[token[i][0]], token[i][1])
    for q in tick:
        g.wait_ge(T.sem["q" + q], tick[q])


def rank_program(g, core, T, topo):
    if T.rank_of(core) is None:
        return
    emit(g, T, build(T, topo, core))
